import numpy as np
import ml_dtypes


def mxq(x, axis, fmt="e4m3"):
    dtype, down = {"e4m3": (ml_dtypes.float8_e4m3fn, 7), "e5m2": (ml_dtypes.float8_e5m2, 14)}[fmt]
    v = np.moveaxis(np.asarray(x, np.float32).astype(ml_dtypes.bfloat16).astype(np.float64), axis, -1)
    blocks = v.reshape(v.shape[:-1] + (-1, 32))
    amax = np.abs(blocks).max(-1, keepdims=True)
    byte = np.maximum(np.where(amax > 0, np.frexp(amax)[1] - 1 + 127, 0) - down, 1)
    scale = np.exp2(byte - 127.0)
    codes = (blocks / scale).astype(np.float32).astype(dtype).astype(np.float64)
    return np.moveaxis((codes * scale).reshape(v.shape), -1, axis)


WIDE = False


def mx_kscale(k):
    if not WIDE:
        return np.ones(k)
    levels = np.array([10, -10, 5, -5, 0])
    if k % 512:
        return np.exp2(np.random.permutation(np.resize(levels, k // 32))).repeat(32)
    a = np.empty((k // 512, 16))
    for p in range(k // 512):
        a[p, :8] = np.random.permutation(np.resize(levels, 8))
        for g in range(8):
            far = levels[np.abs(levels - a[p, g]) >= 10]
            a[p, g + 8] = far[np.random.randint(len(far))]
    return np.exp2(a.ravel()).repeat(32)


def f64(x):
    return np.asarray(x).astype(np.float64)


def striped(idx):
    return np.tile(idx.reshape(-1, 16).T, (8, 1)).astype(np.uint16)


def unstriped(offs):
    return offs[:16].T.reshape(-1).astype(np.int64)


E2M1 = np.array([0.0, 0.5, 1.0, 1.5, 2.0, 3.0, 4.0, 6.0, -0.0, -0.5, -1.0, -1.5, -2.0, -3.0, -4.0, -6.0])


def pack_weight(w, fmt):
    k, n = w.shape
    w = f64(np.asarray(w, np.float32).astype(ml_dtypes.bfloat16)).reshape(k // 32, 32, n)
    amax = np.abs(w).max(1)
    if fmt == "e4m3":
        byte = np.frexp(amax)[1] - 1 + 127 - 7
    else:
        mant, ex = np.frexp(amax / 6.0)
        byte = np.where(mant > 0.5, ex, ex - 1) + 127
    byte = np.clip(np.where(amax > 0, byte, 1), 1, 254)
    scaled = (w * np.exp2(127.0 - byte)[:, None, :]).reshape(k, n).astype(np.float32)
    by_word = np.ascontiguousarray(scaled.reshape(k // 512, 128, 4, n).transpose(0, 1, 3, 2))
    if fmt == "e4m3":
        words = by_word.astype(ml_dtypes.float8_e4m3fn).view(np.uint8)
    else:
        c = by_word.astype(ml_dtypes.float4_e2m1fn).view(np.uint8) & 0xF
        words = (c[..., 0::2] | (c[..., 1::2] << 4)).reshape(k // 512, 128, 2 * n)
    return np.ascontiguousarray(words), np.ascontiguousarray(byte.astype(np.uint8).reshape(k // 512, 16, n))


def unpack_weight(words, scales, fmt):
    g, _, n = scales.shape
    words = np.ascontiguousarray(words).reshape(g, 128, n, -1)
    if fmt == "e4m3":
        vals = words.view(ml_dtypes.float8_e4m3fn).astype(np.float64)
    else:
        nib = np.empty((g, 128, n, 4), np.uint8)
        nib[..., 0::2] = words & 0xF
        nib[..., 1::2] = words >> 4
        vals = E2M1[nib]
    vals = vals * np.repeat(np.exp2(scales.astype(np.float64) - 127.0), 8, axis=1)[..., None]
    return vals.transpose(0, 1, 3, 2).reshape(g * 512, n)


def silu(v):
    return v / (1.0 + np.exp(-np.maximum(v, -700.0)))


K, T, E, C, H, N = 512, 512, 4, 256, 512, 256


def by_expert(wq, xq):
    return np.concatenate([wq[e].T @ xq[:, e * C:(e + 1) * C] for e in range(E)], axis=1)


def setup_inputs():
    n = np.random.standard_normal
    s = mx_kscale(K)
    u = mx_kscale(H)
    first = np.random.permutation(np.repeat(np.arange(E), T // E))
    second = (first + 1 + np.random.permutation(np.repeat(np.arange(E - 1), -(-T // (E - 1)))[:T])) % E
    while np.bincount(second, minlength=E).max() != T // E:
        load = np.bincount(second, minlength=E); hi, lo = int(load.argmax()), int(load.argmin())
        t = np.flatnonzero((second == hi) & (first != lo))[0]; second[t] = lo
    slot_token = np.empty(E * C, np.int64); pos = np.empty((2, T), np.int64); fill = np.zeros(E, np.int64)
    place = np.stack([np.random.permutation(C) for _ in range(E)])
    for r, deal in enumerate((first, second)):
        for t in np.random.permutation(T):
            e = deal[t]; j = e * C + place[e, fill[e]]; fill[e] += 1; slot_token[j] = t; pos[r, t] = j
    g = np.random.uniform(0.2, 0.8, T)
    x = pack_weight(n((K, T)) * s[:, None], "e4m3")
    w = [pack_weight(m, "e2m1") for m in n((E, K, N)) / np.sqrt(K) / s[None, :, None]]
    wb = [pack_weight(m, "e4m3") for m in n((E, H, N)) / np.sqrt(H) / u[None, :, None]]
    return {
        "x_words": x[0],
        "x_scales": x[1],
        "w_words": np.stack([m[0] for m in w]),
        "w_scales": np.stack([m[1] for m in w]),
        "wa": (n((E, K, H)) / np.sqrt(K) / s[None, :, None] * u).astype(np.float32),
        "wb_words": np.stack([m[0] for m in wb]),
        "wb_scales": np.stack([m[1] for m in wb]),
        "gate": np.stack([np.tile(g, (128, 1)), np.tile(1.0 - g, (128, 1))]).astype(np.float32),
        "offs": striped(slot_token),
        "pos1": striped(pos[0]),
        "pos2": striped(pos[1]),
    }


def reference(x_words, x_scales, w_words, w_scales, wa, wb_words, wb_scales, gate, offs, pos1, pos2):
    w = np.stack([unpack_weight(w_words[e], w_scales[e], "e2m1") for e in range(E)])
    waq = mxq(f64(wa), 1, "e4m3")
    wb = np.stack([unpack_weight(wb_words[e], wb_scales[e], "e4m3") for e in range(E)])
    idx = unstriped(offs)
    xq = unpack_weight(x_words, x_scales, "e4m3")[:, idx]
    h = silu(by_expert(waq, xq))
    y = by_expert(w, xq) + by_expert(wb, mxq(h, 0, "e4m3"))
    out = sum(f64(gate[r, :1]) * y[:, unstriped(p)] for r, p in enumerate((pos1, pos2)))
    return out

@@ -1,0 +1,205 @@
+from contextlib import ExitStack
+
+import concourse.mybir as mybir
+
+K, T, E, C, H, N = 512, 512, 4, 256, 512, 256
+FLOPS = 2 * E * C * (K * H + K * N + H * N)
+
+F32 = mybir.dt.float32
+BF16 = mybir.dt.bfloat16
+I32 = mybir.dt.int32
+U32 = mybir.dt.uint32
+U16 = mybir.dt.uint16
+U8 = mybir.dt.uint8
+FP8X4 = mybir.dt.float8_e4m3fn_x4
+FP4X4 = mybir.dt.float4_e2m1fn_x4
+SILU = mybir.ActivationFunctionType.Silu
+MULT = mybir.AluOpType.mult
+ADD = mybir.AluOpType.add
+
+P = 128
+S = E * C
+RAW_BYTES = 4 * H * 4
+VECTOR_M = (48, 40, 92, 92)
+
+
+def tile_moe_elr_silu_kernel(tc, x_words, x_scales, w_words, w_scales, wa, wb_words, wb_scales, gate, offs, pos1, pos2, out):
+    nc = tc.nc
+    with ExitStack() as ctx:
+        keep = ctx.enter_context(tc.tile_pool(name="keep", bufs=1))
+        shared = ctx.enter_context(tc.tile_pool(name="shared", bufs=1))
+        psum = ctx.enter_context(tc.psum_pool(name="psum", bufs=1))
+
+        def kept(shape, dtype, name):
+            return keep.tile(shape, dtype, name=name, align_bytes=64)
+
+        def placed(shape, dtype, name, offset):
+            return shared.tile(shape, dtype, name=name, align_bytes=64, offset=offset)
+
+        offs_t = keep.tile([P, S // 16], U16, name="offs_t")
+        pos_t = [keep.tile([P, T // 16], U16, name="pos%d" % r) for r in range(2)]
+        xw = kept([P, T], I32, "xw")
+        xs = kept([P, T], U8, "xs")
+        raw = [placed([P, 4, H], F32, "raw%d" % e, e * RAW_BYTES) for e in range(E)]
+        gw = [kept([P, C], U32, "gw%d" % e) for e in range(3)] + [placed([P, C], U32, "gw3", 0)]
+        gs = [kept([P, C], U8, "gs%d" % e) for e in range(3)] + [placed([P, C], U8, "gs3", 4 * C)]
+        wab = [kept([P, 4, P, 4], BF16, "wab%d" % e) for e in range(E)]
+        waq = kept([P, E, H], U32, "waq")
+        was = kept([P, E, H], U8, "was")
+        wt = kept([P, E, 2 * N], U8, "wt")
+        wst = kept([P, E, N], U8, "wst")
+        wbt = kept([P, E, N], I32, "wbt")
+        wbst = kept([P, E, N], U8, "wbst")
+        gt = kept([P, 2, T], F32, "gt")
+        hb = [placed([P, C, 4], BF16, "hb2", 3 * RAW_BYTES + 4 * C) if e == 2 else kept([P, C, 4], BF16, "hb%d" % e) for e in range(E)]
+        hq = [placed([P, C], U32, "hq1", 3 * RAW_BYTES) if e == 1 else kept([P, C], U32, "hq%d" % e) for e in range(E)]
+        hs = kept([P, S], U8, "hs")
+        y = [kept([P, S], F32, "y%d" % f) for f in range(2)]
+        warm = keep.tile([P, 8], F32, name="warm")
+        warm2 = keep.tile([P, 8], F32, name="warm2")
+
+        nc.gpsimd.memset(wbst[:].bitcast(I32), 0)
+        nc.gpsimd.memset(wst[:].bitcast(I32), 0)
+        nc.vector.memset(warm[:], 0.0)
+        nc.scalar.activation(warm2[:], warm[:], SILU)
+
+        nc.sync.dma_start(offs_t[:], offs)
+        nc.sync.dma_start(xw[:], x_words[0].rearrange("p t d -> p (t d)").bitcast(I32))
+        for q in range(4):
+            nc.sync.dma_start(
+                xs[32 * q : 32 * q + 32].bitcast(I32),
+                x_scales[0, 4 * q : 4 * q + 4, :].bitcast(I32).unsqueeze(0).broadcast_to([8, 4, T // 4]),
+            )
+        for plane, scales in ((wbst, wb_scales), (wst, w_scales)):
+            for q in range(4):
+                nc.gpsimd.dma_start(
+                    plane[32 * q : 32 * q + 4].bitcast(I32),
+                    scales[:, 0, 4 * q : 4 * q + 4, :].bitcast(I32).rearrange("e r n -> r e n"),
+                )
+        for e in range(E):
+            nc.sync.dma_start(raw[e][:], wa[e].rearrange("(p j) i -> p j i", j=4))
+        for e0 in (0, 2):
+            nc.sync.dma_start(
+                wt[:, e0 : e0 + 2, :].bitcast(I32),
+                w_words[e0 : e0 + 2, 0].bitcast(I32).rearrange("e p b -> p e b"),
+            )
+            nc.sync.dma_start(
+                wbt[:, e0 : e0 + 2, :],
+                wb_words[e0 : e0 + 2, 0].rearrange("e p n d -> p e (n d)").bitcast(I32),
+            )
+        nc.sync.dma_start(gt[:], gate.rearrange("r p t -> p r t"))
+        nc.sync.dma_start(pos_t[0][:], pos1)
+        nc.sync.dma_start(pos_t[1][:], pos2)
+
+        def gather(e):
+            lst = offs_t[:, e * C // 16 : (e + 1) * C // 16]
+            nc.vector.tensor_copy(gw[e][:], xw[:].bitcast(U32).indirect(lst))
+            nc.vector.tensor_copy(gs[e][:], xs[:].indirect(lst))
+
+        def cast(e):
+            for engine_copy, m0, m1 in ((nc.vector.tensor_copy, 0, VECTOR_M[e]), (nc.scalar.copy, VECTOR_M[e], P)):
+                engine_copy(
+                    wab[e][:, :, m0:m1, :].rearrange("p t m j -> p m j t"),
+                    raw[e][:, :, 4 * m0 : 4 * m1].rearrange("p j (m t) -> p m j t", t=4),
+                )
+
+        def quant_wa(e, t0, t1):
+            nc.vector.quantize_mx(
+                out=waq[:, e, t0 * P : t1 * P].bitcast(FP8X4),
+                scales=was[:, e, t0 * P : t1 * P],
+                in_=wab[e][:, t0:t1].rearrange("p t m j -> p (t m j)"),
+            )
+
+        def first_layer(e):
+            for a in range(2):
+                cols = slice(a * P, (a + 1) * P)
+                bank = psum.tile([P, 4, P], F32, name="h%d" % a)
+                for t in range(4):
+                    nc.tensor.matmul_mx(
+                        out=bank[:, t, :],
+                        lhsT=waq[:, e, t * P : (t + 1) * P].bitcast(FP8X4),
+                        lhsT_scale=was[:, e, t * P : (t + 1) * P],
+                        rhs=gw[e][:, cols].bitcast(FP8X4),
+                        rhs_scale=gs[e][:, cols],
+                        start=True,
+                        stop=True,
+                    )
+                nc.scalar.activation(hb[e][:, cols, :], bank[:].rearrange("p t s -> p s t"), SILU)
+
+        def quant_h(e, s0, s1):
+            nc.vector.quantize_mx(
+                out=hq[e][:, s0:s1].bitcast(FP8X4),
+                scales=hs[:, e * C + s0 : e * C + s1],
+                in_=hb[e][:, s0:s1, :].rearrange("p s t -> p (s t)"),
+            )
+
+        def second_layer(e, f, a, acc):
+            cols = slice(a * P, (a + 1) * P)
+            nc.tensor.matmul_mx(
+                out=acc,
+                lhsT=wbt[:, e, f * P : (f + 1) * P].bitcast(FP8X4),
+                lhsT_scale=wbst[:, e, f * P : (f + 1) * P],
+                rhs=hq[e][:, cols].bitcast(FP8X4),
+                rhs_scale=hs[:, e * C + a * P : e * C + (a + 1) * P],
+                start=True,
+                stop=False,
+            )
+            nc.tensor.matmul_mx(
+                out=acc,
+                lhsT=wt[:, e, 2 * f * P : 2 * (f + 1) * P].bitcast(FP4X4),
+                lhsT_scale=wst[:, e, f * P : (f + 1) * P],
+                rhs=gw[e][:, cols].bitcast(FP8X4),
+                rhs_scale=gs[e][:, cols],
+                start=False,
+                stop=True,
+            )
+
+        def results(e, f, engine_copy):
+            bank = psum.tile([P, C], F32, name="y%d" % e)
+            for a in range(2):
+                second_layer(e, f, a, bank[:, a * P : (a + 1) * P])
+            engine_copy(y[f][:, e * C : (e + 1) * C], bank[:])
+
+        for e in range(3):
+            gather(e)
+        cast(0)
+        quant_wa(0, 0, 4)
+        first_layer(0)
+        gather(3)
+        cast(1)
+        quant_wa(1, 0, 4)
+        first_layer(1)
+        cast(2)
+        quant_h(0, 0, C)
+        quant_wa(2, 0, 4)
+        cast(3)
+        for t in range(4):
+            quant_wa(3, t, t + 1)
+        first_layer(2)
+        first_layer(3)
+        quant_h(1, 0, C)
+        quant_h(2, 0, C)
+        quant_h(3, 0, P)
+        quant_h(3, P, C)
+        results(0, 0, nc.vector.tensor_copy)
+        results(1, 0, nc.scalar.copy)
+        results(2, 0, nc.vector.tensor_copy)
+        for a, name in enumerate(("y3", "y3b")):
+            bank = psum.tile([P, P], F32, name=name)
+            second_layer(3, 0, a, bank[:])
+            nc.scalar.copy(y[0][:, 3 * C + a * P : 3 * C + (a + 1) * P], bank[:])
+        for e in range(E):
+            results(e, 1, nc.scalar.copy)
+
+        half = T // 2
+        for f in range(2):
+            first = kept([P, T], F32, "first%d" % f)
+            nc.vector.tensor_tensor(first[:], y[f][:].indirect(pos_t[0][:]), gt[:, 0, :], MULT)
+            second = [kept([P, half], F32, "second%d" % b) for b in range(2)]
+            for b in range(2):
+                lst = pos_t[1][:, b * half // 16 : (b + 1) * half // 16]
+                nc.vector.tensor_tensor(second[b][:], y[f][:].indirect(lst), gt[:, 1, b * half : (b + 1) * half], MULT)
+            for b in range(2):
+                res = kept([P, half], F32, "res%d_%d" % (f, b))
+                nc.vector.tensor_tensor(res[:], first[:, b * half : (b + 1) * half], second[b][:], ADD)
+                nc.sync.dma_start(out[f * P : (f + 1) * P, b * half : (b + 1) * half], res[:])

@@ -19,8 +19,8 @@ ADD = mybir.AluOpType.add
 
 P = 128
 S = E * C
-RAW_BYTES = 4 * H * 4
-VECTOR_M = (48, 40, 92, 92)
+HALF = P // 2
+VECTOR_M = (20, 32, 60, 64, 32)
 
 
 def tile_moe_elr_silu_kernel(tc, x_words, x_scales, w_words, w_scales, wa, wb_words, wb_scales, gate, offs, pos1, pos2, out):
@@ -40,55 +40,64 @@ def tile_moe_elr_silu_kernel(tc, x_words, x_scales, w_words, w_scales, wa, wb_wo
         pos_t = [keep.tile([P, T // 16], U16, name="pos%d" % r) for r in range(2)]
         xw = kept([P, T], I32, "xw")
         xs = kept([P, T], U8, "xs")
-        raw = [placed([P, 4, H], F32, "raw%d" % e, e * RAW_BYTES) for e in range(E)]
-        gw = [kept([P, C], U32, "gw%d" % e) for e in range(3)] + [placed([P, C], U32, "gw3", 0)]
-        gs = [kept([P, C], U8, "gs%d" % e) for e in range(3)] + [placed([P, C], U8, "gs3", 4 * C)]
+        raw = [placed([P, 4, H], F32, "raw0", 0)] + [kept([P, 4, H], F32, "raw%d" % e) for e in range(1, E - 1)]
+        raw_last = [kept([P, 4, H // 2], F32, "raw_last%d" % u) for u in range(2)]
+        gw = [kept([P, C], U32, "gw%d" % e) for e in range(E - 1)] + [placed([P, C], U32, "gw3", 0)]
+        gs = [kept([P, C], U8, "gs%d" % e) for e in range(E - 1)] + [placed([P, C], U8, "gs3", 4 * C)]
         wab = [kept([P, 4, P, 4], BF16, "wab%d" % e) for e in range(E)]
         waq = kept([P, E, H], U32, "waq")
         was = kept([P, E, H], U8, "was")
         wt = kept([P, E, 2 * N], U8, "wt")
         wst = kept([P, E, N], U8, "wst")
         wbt = kept([P, E, N], I32, "wbt")
-        wbst = kept([P, E, N], U8, "wbst")
+        wbst = kept([P, N], U8, "wbst")
         gt = kept([P, 2, T], F32, "gt")
-        hb = [placed([P, C, 4], BF16, "hb2", 3 * RAW_BYTES + 4 * C) if e == 2 else kept([P, C, 4], BF16, "hb%d" % e) for e in range(E)]
-        hq = [placed([P, C], U32, "hq1", 3 * RAW_BYTES) if e == 1 else kept([P, C], U32, "hq%d" % e) for e in range(E)]
+        hb = [kept([P, C, 4], BF16, "hb%d" % e) for e in range(E)]
+        hq = [kept([P, C], U32, "hq%d" % e) for e in range(E)]
         hs = kept([P, S], U8, "hs")
         y = [kept([P, S], F32, "y%d" % f) for f in range(2)]
         warm = keep.tile([P, 8], F32, name="warm")
         warm2 = keep.tile([P, 8], F32, name="warm2")
 
-        nc.gpsimd.memset(wbst[:].bitcast(I32), 0)
+        nc.vector.memset(wbst[:].bitcast(I32), 0)
         nc.gpsimd.memset(wst[:].bitcast(I32), 0)
         nc.vector.memset(warm[:], 0.0)
-        nc.scalar.activation(warm2[:], warm[:], SILU)
+
+        def load_wa(dst, e, c0, c1):
+            nc.sync.dma_start(dst[:], wa[e].rearrange("(p j) i -> p j i", j=4)[:, :, c0:c1])
 
         nc.sync.dma_start(offs_t[:], offs)
         nc.sync.dma_start(xw[:], x_words[0].rearrange("p t d -> p (t d)").bitcast(I32))
         for q in range(4):
-            nc.sync.dma_start(
+            nc.scalar.dma_start(
                 xs[32 * q : 32 * q + 32].bitcast(I32),
                 x_scales[0, 4 * q : 4 * q + 4, :].bitcast(I32).unsqueeze(0).broadcast_to([8, 4, T // 4]),
             )
-        for plane, scales in ((wbst, wb_scales), (wst, w_scales)):
-            for q in range(4):
-                nc.gpsimd.dma_start(
-                    plane[32 * q : 32 * q + 4].bitcast(I32),
-                    scales[:, 0, 4 * q : 4 * q + 4, :].bitcast(I32).rearrange("e r n -> r e n"),
-                )
-        for e in range(E):
-            nc.sync.dma_start(raw[e][:], wa[e].rearrange("(p j) i -> p j i", j=4))
-        for e0 in (0, 2):
-            nc.sync.dma_start(
-                wt[:, e0 : e0 + 2, :].bitcast(I32),
-                w_words[e0 : e0 + 2, 0].bitcast(I32).rearrange("e p b -> p e b"),
+        for q in range(4):
+            nc.scalar.dma_start(
+                wbst[32 * q : 32 * q + 16].bitcast(I32),
+                wb_scales[:, 0, 4 * q : 4 * q + 4, :].bitcast(I32),
             )
+            nc.gpsimd.dma_start(
+                wst[32 * q : 32 * q + 4].bitcast(I32),
+                w_scales[:, 0, 4 * q : 4 * q + 4, :].bitcast(I32).rearrange("e r n -> r e n"),
+            )
+        nc.scalar.activation(warm2[:], warm[:], SILU)
+        for e in range(E - 1):
+            load_wa(raw[e], e, 0, H)
+        load_wa(raw_last[0], 3, 0, H // 2)
+        load_wa(raw_last[1], 3, H // 2, H)
+        for e0 in (0, 2):
             nc.sync.dma_start(
                 wbt[:, e0 : e0 + 2, :],
                 wb_words[e0 : e0 + 2, 0].rearrange("e p n d -> p e (n d)").bitcast(I32),
             )
-        nc.sync.dma_start(gt[:], gate.rearrange("r p t -> p r t"))
+            nc.sync.dma_start(
+                wt[:, e0 : e0 + 2, :].bitcast(I32),
+                w_words[e0 : e0 + 2, 0].bitcast(I32).rearrange("e p b -> p e b"),
+            )
         nc.sync.dma_start(pos_t[0][:], pos1)
+        nc.sync.dma_start(gt[:], gate.rearrange("r p t -> p r t"))
         nc.sync.dma_start(pos_t[1][:], pos2)
 
         def gather(e):
@@ -96,24 +105,40 @@ def tile_moe_elr_silu_kernel(tc, x_words, x_scales, w_words, w_scales, wa, wb_wo
             nc.vector.tensor_copy(gw[e][:], xw[:].bitcast(U32).indirect(lst))
             nc.vector.tensor_copy(gs[e][:], xs[:].indirect(lst))
 
-        def cast(e):
-            for engine_copy, m0, m1 in ((nc.vector.tensor_copy, 0, VECTOR_M[e]), (nc.scalar.copy, VECTOR_M[e], P)):
+        def cast(engine_copy, e, src, base, m0, m1):
+            if m1 > m0:
                 engine_copy(
                     wab[e][:, :, m0:m1, :].rearrange("p t m j -> p m j t"),
-                    raw[e][:, :, 4 * m0 : 4 * m1].rearrange("p j (m t) -> p m j t", t=4),
+                    src[:, :, 4 * (m0 - base) : 4 * (m1 - base)].rearrange("p j (m t) -> p m j t", t=4),
                 )
 
-        def quant_wa(e, t0, t1):
+        def cast_pair(e, src, base, width, share):
+            cast(nc.vector.tensor_copy, e, src, base, base, base + share)
+            cast(nc.scalar.copy, e, src, base, base + share, base + width)
+
+        def quant_wa(e):
             nc.vector.quantize_mx(
-                out=waq[:, e, t0 * P : t1 * P].bitcast(FP8X4),
-                scales=was[:, e, t0 * P : t1 * P],
-                in_=wab[e][:, t0:t1].rearrange("p t m j -> p (t m j)"),
+                out=waq[:, e, :].bitcast(FP8X4),
+                scales=was[:, e, :],
+                in_=wab[e][:].rearrange("p t m j -> p (t m j)"),
             )
+
+        def quant_wa_half(e, u):
+            for t in range(4):
+                cols = slice(t * P + u * HALF, t * P + (u + 1) * HALF)
+                nc.vector.quantize_mx(
+                    out=waq[:, e, cols].bitcast(FP8X4),
+                    scales=was[:, e, cols],
+                    in_=wab[e][:, t, u * HALF : (u + 1) * HALF, :].rearrange("p m j -> p (m j)"),
+                )
+
+        banks = {}
 
         def first_layer(e):
             for a in range(2):
                 cols = slice(a * P, (a + 1) * P)
-                bank = psum.tile([P, 4, P], F32, name="h%d" % a)
+                bank = psum.tile([P, 4, P], F32, name="h%d" % (2 * (e % 2) + a))
+                banks[e, a] = bank
                 for t in range(4):
                     nc.tensor.matmul_mx(
                         out=bank[:, t, :],
@@ -124,7 +149,10 @@ def tile_moe_elr_silu_kernel(tc, x_words, x_scales, w_words, w_scales, wa, wb_wo
                         start=True,
                         stop=True,
                     )
-                nc.scalar.activation(hb[e][:, cols, :], bank[:].rearrange("p t s -> p s t"), SILU)
+
+        def silu(e):
+            for a in range(2):
+                nc.scalar.activation(hb[e][:, a * P : (a + 1) * P, :], banks[e, a][:].rearrange("p t s -> p s t"), SILU)
 
         def quant_h(e, s0, s1):
             nc.vector.quantize_mx(
@@ -133,63 +161,70 @@ def tile_moe_elr_silu_kernel(tc, x_words, x_scales, w_words, w_scales, wa, wb_wo
                 in_=hb[e][:, s0:s1, :].rearrange("p s t -> p (s t)"),
             )
 
-        def second_layer(e, f, a, acc):
+        def frozen(e, f, a, acc):
             cols = slice(a * P, (a + 1) * P)
-            nc.tensor.matmul_mx(
-                out=acc,
-                lhsT=wbt[:, e, f * P : (f + 1) * P].bitcast(FP8X4),
-                lhsT_scale=wbst[:, e, f * P : (f + 1) * P],
-                rhs=hq[e][:, cols].bitcast(FP8X4),
-                rhs_scale=hs[:, e * C + a * P : e * C + (a + 1) * P],
-                start=True,
-                stop=False,
-            )
             nc.tensor.matmul_mx(
                 out=acc,
                 lhsT=wt[:, e, 2 * f * P : 2 * (f + 1) * P].bitcast(FP4X4),
                 lhsT_scale=wst[:, e, f * P : (f + 1) * P],
                 rhs=gw[e][:, cols].bitcast(FP8X4),
                 rhs_scale=gs[e][:, cols],
+                start=True,
+                stop=False,
+            )
+
+        def adapter(e, f, a, acc):
+            cols = slice(a * P, (a + 1) * P)
+            nc.tensor.matmul_mx(
+                out=acc,
+                lhsT=wbt[:, e, f * P : (f + 1) * P].bitcast(FP8X4),
+                lhsT_scale=wbst[4 * e :, f * P : (f + 1) * P],
+                rhs=hq[e][:, cols].bitcast(FP8X4),
+                rhs_scale=hs[:, e * C + a * P : e * C + (a + 1) * P],
                 start=False,
                 stop=True,
             )
 
-        def results(e, f, engine_copy):
-            bank = psum.tile([P, C], F32, name="y%d" % e)
-            for a in range(2):
-                second_layer(e, f, a, bank[:, a * P : (a + 1) * P])
-            engine_copy(y[f][:, e * C : (e + 1) * C], bank[:])
+        def results(name, f, b0, b1, engine_copy):
+            bank = psum.tile([P, (b1 - b0) * P], F32, name=name)
+            for b in range(b0, b1):
+                acc = bank[:, (b - b0) * P : (b - b0 + 1) * P]
+                frozen(b // 2, f, b % 2, acc)
+                adapter(b // 2, f, b % 2, acc)
+            engine_copy(y[f][:, b0 * P : b1 * P], bank[:])
 
-        for e in range(3):
+        for e in range(E - 1):
             gather(e)
-        cast(0)
-        quant_wa(0, 0, 4)
+        cast_pair(0, raw[0], 0, P, VECTOR_M[0])
+        quant_wa(0)
         first_layer(0)
         gather(3)
-        cast(1)
-        quant_wa(1, 0, 4)
+        cast_pair(1, raw[1], 0, P, VECTOR_M[1])
+        silu(0)
+        quant_wa(1)
         first_layer(1)
-        cast(2)
-        quant_h(0, 0, C)
-        quant_wa(2, 0, 4)
-        cast(3)
-        for t in range(4):
-            quant_wa(3, t, t + 1)
+        cast_pair(2, raw[2], 0, P, VECTOR_M[2])
+        silu(1)
+        quant_wa(2)
         first_layer(2)
+        cast_pair(3, raw_last[0], 0, HALF, VECTOR_M[3])
+        quant_wa_half(3, 0)
+        cast_pair(3, raw_last[1], HALF, HALF, VECTOR_M[4])
+        quant_wa_half(3, 1)
+        silu(2)
         first_layer(3)
+        silu(3)
+        quant_h(0, 0, C)
         quant_h(1, 0, C)
+        results("ya", 0, 0, 4, nc.vector.tensor_copy)
         quant_h(2, 0, C)
         quant_h(3, 0, P)
         quant_h(3, P, C)
-        results(0, 0, nc.vector.tensor_copy)
-        results(1, 0, nc.scalar.copy)
-        results(2, 0, nc.vector.tensor_copy)
-        for a, name in enumerate(("y3", "y3b")):
-            bank = psum.tile([P, P], F32, name=name)
-            second_layer(3, 0, a, bank[:])
-            nc.scalar.copy(y[0][:, 3 * C + a * P : 3 * C + (a + 1) * P], bank[:])
-        for e in range(E):
-            results(e, 1, nc.scalar.copy)
+        results("yb", 0, 4, 6, nc.vector.tensor_copy)
+        results("yc", 0, 6, 7, nc.scalar.copy)
+        results("yd", 0, 7, 8, nc.scalar.copy)
+        results("yc", 1, 0, 4, nc.scalar.copy)
+        results("yd", 1, 4, 8, nc.scalar.copy)
 
         half = T // 2
         for f in range(2):

@@ -59,7 +59,7 @@ def tile_moe_elr_silu_kernel(tc, x_words, x_scales, w_words, w_scales, wa, wb_wo
         warm = keep.tile([P, 8], F32, name="warm")
         warm2 = keep.tile([P, 8], F32, name="warm2")
 
-        nc.vector.memset(wbst[:].bitcast(I32), 0)
+        nc.gpsimd.memset(wbst[:].bitcast(I32), 0)
         nc.gpsimd.memset(wst[:].bitcast(I32), 0)
         nc.vector.memset(warm[:], 0.0)
 
@@ -74,7 +74,7 @@ def tile_moe_elr_silu_kernel(tc, x_words, x_scales, w_words, w_scales, wa, wb_wo
                 x_scales[0, 4 * q : 4 * q + 4, :].bitcast(I32).unsqueeze(0).broadcast_to([8, 4, T // 4]),
             )
         for q in range(4):
-            nc.scalar.dma_start(
+            nc.gpsimd.dma_start(
                 wbst[32 * q : 32 * q + 16].bitcast(I32),
                 wb_scales[:, 0, 4 * q : 4 * q + 4, :].bitcast(I32),
             )
@@ -150,6 +150,19 @@ def tile_moe_elr_silu_kernel(tc, x_words, x_scales, w_words, w_scales, wa, wb_wo
                         stop=True,
                     )
 
+        def keep_clock(e, passes):
+            spare = psum.tile([P, 2, C], F32, name="ya")
+            for t in range(passes):
+                nc.tensor.matmul_mx(
+                    out=spare[:, t % 2, :],
+                    lhsT=waq[:, e, t * P : (t + 1) * P].bitcast(FP8X4),
+                    lhsT_scale=was[:, e, t * P : (t + 1) * P],
+                    rhs=gw[e][:].bitcast(FP8X4),
+                    rhs_scale=gs[e][:],
+                    start=True,
+                    stop=True,
+                )
+
         def silu(e):
             for a in range(2):
                 nc.scalar.activation(hb[e][:, a * P : (a + 1) * P, :], banks[e, a][:].rearrange("p t s -> p s t"), SILU)
@@ -198,15 +211,18 @@ def tile_moe_elr_silu_kernel(tc, x_words, x_scales, w_words, w_scales, wa, wb_wo
         cast_pair(0, raw[0], 0, P, VECTOR_M[0])
         quant_wa(0)
         first_layer(0)
+        keep_clock(0, 3)
         gather(3)
         cast_pair(1, raw[1], 0, P, VECTOR_M[1])
         silu(0)
         quant_wa(1)
         first_layer(1)
+        keep_clock(1, 2)
         cast_pair(2, raw[2], 0, P, VECTOR_M[2])
         silu(1)
         quant_wa(2)
         first_layer(2)
+        keep_clock(2, 2)
         cast_pair(3, raw_last[0], 0, HALF, VECTOR_M[3])
         quant_wa_half(3, 0)
         cast_pair(3, raw_last[1], HALF, HALF, VECTOR_M[4])

@@ -20,7 +20,7 @@ ADD = mybir.AluOpType.add
 P = 128
 S = E * C
 HALF = P // 2
-VECTOR_M = (20, 32, 60, 64, 32)
+VECTOR_M = (44, 52, 52, 60, 60)
 
 
 def tile_moe_elr_silu_kernel(tc, x_words, x_scales, w_words, w_scales, wa, wb_words, wb_scales, gate, offs, pos1, pos2, out):
@@ -69,7 +69,7 @@ def tile_moe_elr_silu_kernel(tc, x_words, x_scales, w_words, w_scales, wa, wb_wo
         nc.sync.dma_start(offs_t[:], offs)
         nc.sync.dma_start(xw[:], x_words[0].rearrange("p t d -> p (t d)").bitcast(I32))
         for q in range(4):
-            nc.scalar.dma_start(
+            nc.sync.dma_start(
                 xs[32 * q : 32 * q + 32].bitcast(I32),
                 x_scales[0, 4 * q : 4 * q + 4, :].bitcast(I32).unsqueeze(0).broadcast_to([8, 4, T // 4]),
             )

@@ -1,6 +1,7 @@
 from contextlib import ExitStack
 
 import concourse.mybir as mybir
+from concourse.masks import make_identity
 
 K, T, E, C, H, N = 512, 512, 4, 256, 512, 256
 FLOPS = 2 * E * C * (K * H + K * N + H * N)
@@ -56,12 +57,14 @@ def tile_moe_elr_silu_kernel(tc, x_words, x_scales, w_words, w_scales, wa, wb_wo
         hq = [kept([P, C], U32, "hq%d" % e) for e in range(E)]
         hs = kept([P, S], U8, "hs")
         y = [kept([P, S], F32, "y%d" % f) for f in range(2)]
+        ident = kept([P, P], F32, "ident")
         warm = keep.tile([P, 8], F32, name="warm")
         warm2 = keep.tile([P, 8], F32, name="warm2")
 
         nc.gpsimd.memset(wbst[:].bitcast(I32), 0)
         nc.gpsimd.memset(wst[:].bitcast(I32), 0)
         nc.vector.memset(warm[:], 0.0)
+        make_identity(nc, ident[:])
 
         def load_wa(dst, e, c0, c1):
             nc.sync.dma_start(dst[:], wa[e].rearrange("(p j) i -> p j i", j=4)[:, :, c0:c1])
@@ -78,24 +81,18 @@ def tile_moe_elr_silu_kernel(tc, x_words, x_scales, w_words, w_scales, wa, wb_wo
                 wbst[32 * q : 32 * q + 16].bitcast(I32),
                 wb_scales[:, 0, 4 * q : 4 * q + 4, :].bitcast(I32),
             )
-            nc.gpsimd.dma_start(
-                wst[32 * q : 32 * q + 4].bitcast(I32),
-                w_scales[:, 0, 4 * q : 4 * q + 4, :].bitcast(I32).rearrange("e r n -> r e n"),
-            )
         nc.scalar.activation(warm2[:], warm[:], SILU)
         for e in range(E - 1):
             load_wa(raw[e], e, 0, H)
         load_wa(raw_last[0], 3, 0, H // 2)
         load_wa(raw_last[1], 3, H // 2, H)
-        for e0 in (0, 2):
+        for q in range(4):
             nc.sync.dma_start(
-                wbt[:, e0 : e0 + 2, :],
-                wb_words[e0 : e0 + 2, 0].rearrange("e p n d -> p e (n d)").bitcast(I32),
+                wst[32 * q : 32 * q + 4].bitcast(I32),
+                w_scales[:, 0, 4 * q : 4 * q + 4, :].bitcast(I32).rearrange("e r n -> r e n"),
             )
-            nc.sync.dma_start(
-                wt[:, e0 : e0 + 2, :].bitcast(I32),
-                w_words[e0 : e0 + 2, 0].bitcast(I32).rearrange("e p b -> p e b"),
-            )
+        nc.sync.dma_start(wbt[:], wb_words[:, 0].rearrange("e p n d -> p e (n d)").bitcast(I32))
+        nc.sync.dma_start(wt[:].bitcast(I32), w_words[:, 0].bitcast(I32).rearrange("e p b -> p e b"))
         nc.sync.dma_start(pos_t[0][:], pos1)
         nc.sync.dma_start(gt[:], gate.rearrange("r p t -> p r t"))
         nc.sync.dma_start(pos_t[1][:], pos2)
@@ -232,10 +229,10 @@ def tile_moe_elr_silu_kernel(tc, x_words, x_scales, w_words, w_scales, wa, wb_wo
         silu(3)
         quant_h(0, 0, C)
         quant_h(1, 0, C)
-        results("ya", 0, 0, 4, nc.vector.tensor_copy)
         quant_h(2, 0, C)
         quant_h(3, 0, P)
         quant_h(3, P, C)
+        results("ya", 0, 0, 4, nc.scalar.copy)
         results("yb", 0, 4, 6, nc.vector.tensor_copy)
         results("yc", 0, 6, 7, nc.scalar.copy)
         results("yd", 0, 7, 8, nc.scalar.copy)
@@ -243,14 +240,35 @@ def tile_moe_elr_silu_kernel(tc, x_words, x_scales, w_words, w_scales, wa, wb_wo
         results("yd", 1, 4, 8, nc.scalar.copy)
 
         half = T // 2
+
+        def add_on_vector(first, second, res):
+            nc.vector.tensor_tensor(res[:], first, second, ADD)
+
+        def add_on_tensor(first, second, res, b):
+            turned = psum.tile([P, 2, P], F32, name="h%d" % (2 * b))
+            for k in range(2):
+                cols = slice(k * P, (k + 1) * P)
+                nc.tensor.matmul(turned[:, k, :], first[:, cols], ident[:], start=True, stop=False, is_transpose=True)
+                nc.tensor.matmul(turned[:, k, :], second[:, cols], ident[:], start=False, stop=True, is_transpose=True)
+            total = kept([P, 2, P], F32, "total%d" % b)
+            nc.scalar.copy(total[:], turned[:])
+            back = psum.tile([P, 2, P], F32, name="h%d" % (2 * b + 1))
+            for k in range(2):
+                nc.tensor.transpose(back[:, k, :], total[:, k, :], ident[:])
+            nc.scalar.copy(res[:], back[:].rearrange("p k t -> p (k t)"))
+
         for f in range(2):
             first = kept([P, T], F32, "first%d" % f)
             nc.vector.tensor_tensor(first[:], y[f][:].indirect(pos_t[0][:]), gt[:, 0, :], MULT)
-            second = [kept([P, half], F32, "second%d" % b) for b in range(2)]
+            second = [kept([P, half], F32, "second%d_%d" % (f, b)) for b in range(2)]
             for b in range(2):
                 lst = pos_t[1][:, b * half // 16 : (b + 1) * half // 16]
                 nc.vector.tensor_tensor(second[b][:], y[f][:].indirect(lst), gt[:, 1, b * half : (b + 1) * half], MULT)
             for b in range(2):
                 res = kept([P, half], F32, "res%d_%d" % (f, b))
-                nc.vector.tensor_tensor(res[:], first[:, b * half : (b + 1) * half], second[b][:], ADD)
-                nc.sync.dma_start(out[f * P : (f + 1) * P, b * half : (b + 1) * half], res[:])
+                if f == 0:
+                    add_on_tensor(first[:, b * half : (b + 1) * half], second[b][:], res, b)
+                else:
+                    add_on_vector(first[:, b * half : (b + 1) * half], second[b][:], res)
+                queue = nc.scalar if f == 0 else nc.sync
+                queue.dma_start(out[f * P : (f + 1) * P, b * half : (b + 1) * half], res[:])

@@ -14,6 +14,7 @@ U16 = mybir.dt.uint16
 U8 = mybir.dt.uint8
 FP8X4 = mybir.dt.float8_e4m3fn_x4
 FP4X4 = mybir.dt.float4_e2m1fn_x4
+COPY = mybir.ActivationFunctionType.Copy
 SILU = mybir.ActivationFunctionType.Silu
 MULT = mybir.AluOpType.mult
 ADD = mybir.AluOpType.add
@@ -58,6 +59,8 @@ def tile_moe_elr_silu_kernel(tc, x_words, x_scales, w_words, w_scales, wa, wb_wo
         hs = kept([P, S], U8, "hs")
         y = [kept([P, S], F32, "y%d" % f) for f in range(2)]
         ident = kept([P, P], F32, "ident")
+        gate_rows = kept([P, P], F32, "gate_rows")
+        gate_cols = kept([P, 8], F32, "gate_cols")
         warm = keep.tile([P, 8], F32, name="warm")
         warm2 = keep.tile([P, 8], F32, name="warm2")
 
@@ -65,6 +68,7 @@ def tile_moe_elr_silu_kernel(tc, x_words, x_scales, w_words, w_scales, wa, wb_wo
         nc.gpsimd.memset(wst[:].bitcast(I32), 0)
         nc.vector.memset(warm[:], 0.0)
         make_identity(nc, ident[:])
+        nc.gpsimd.memset(gate_rows[:], 0.0)
 
         def load_wa(dst, e, c0, c1):
             nc.sync.dma_start(dst[:], wa[e].rearrange("(p j) i -> p j i", j=4)[:, :, c0:c1])
@@ -94,8 +98,9 @@ def tile_moe_elr_silu_kernel(tc, x_words, x_scales, w_words, w_scales, wa, wb_wo
         nc.sync.dma_start(wbt[:], wb_words[:, 0].rearrange("e p n d -> p e (n d)").bitcast(I32))
         nc.sync.dma_start(wt[:].bitcast(I32), w_words[:, 0].bitcast(I32).rearrange("e p b -> p e b"))
         nc.sync.dma_start(pos_t[0][:], pos1)
-        nc.sync.dma_start(gt[:], gate.rearrange("r p t -> p r t"))
         nc.sync.dma_start(pos_t[1][:], pos2)
+        nc.sync.dma_start(gate_rows[0:8], gate[:, 0, :].rearrange("r (k c) -> r k c", c=P))
+        nc.sync.dma_start(gt[:], gate.rearrange("r p t -> p r t"))
 
         def gather(e):
             lst = offs_t[:, e * C // 16 : (e + 1) * C // 16]
@@ -240,35 +245,39 @@ def tile_moe_elr_silu_kernel(tc, x_words, x_scales, w_words, w_scales, wa, wb_wo
         results("yd", 1, 4, 8, nc.scalar.copy)
 
         half = T // 2
+        turned_gate = psum.tile([P, P], F32, name="ya")
+        nc.tensor.transpose(turned_gate[:], gate_rows[:], ident[:])
+        nc.scalar.copy(gate_cols[:], turned_gate[:, 0:8])
 
-        def add_on_vector(first, second, res):
-            nc.vector.tensor_tensor(res[:], first, second, ADD)
+        def tokens(r, b):
+            return pos_t[r][:, b * half // 16 : (b + 1) * half // 16]
 
-        def add_on_tensor(first, second, res, b):
-            turned = psum.tile([P, 2, P], F32, name="h%d" % (2 * b))
-            for k in range(2):
-                cols = slice(k * P, (k + 1) * P)
-                nc.tensor.matmul(turned[:, k, :], first[:, cols], ident[:], start=True, stop=False, is_transpose=True)
-                nc.tensor.matmul(turned[:, k, :], second[:, cols], ident[:], start=False, stop=True, is_transpose=True)
-            total = kept([P, 2, P], F32, "total%d" % b)
-            nc.scalar.copy(total[:], turned[:])
+        for b in range(2):
+            picked = [kept([P, half], F32, "picked%d_%d" % (r, b)) for r in range(2)]
+            turned = psum.tile([P, 2, 2, P], F32, name="h%d" % (2 * b))
+            scaled = kept([P, 2, 2, P], F32, "scaled%d" % b)
             back = psum.tile([P, 2, P], F32, name="h%d" % (2 * b + 1))
+            res = kept([P, half], F32, "res0_%d" % b)
+            for r in range(2):
+                nc.vector.tensor_copy(picked[r][:], y[0][:].indirect(tokens(r, b)))
+                for k in range(2):
+                    nc.tensor.transpose(turned[:, r, k, :], picked[r][:, k * P : (k + 1) * P], ident[:])
+            for r in range(2):
+                for k in range(2):
+                    col = 4 * r + 2 * b + k
+                    nc.scalar.activation(scaled[:, r, k, :], turned[:, r, k, :], COPY, scale=gate_cols[:, col : col + 1])
             for k in range(2):
-                nc.tensor.transpose(back[:, k, :], total[:, k, :], ident[:])
+                for r in range(2):
+                    nc.tensor.matmul(back[:, k, :], scaled[:, r, k, :], ident[:], start=r == 0, stop=r == 1, is_transpose=True)
             nc.scalar.copy(res[:], back[:].rearrange("p k t -> p (k t)"))
+            nc.scalar.dma_start(out[0:P, b * half : (b + 1) * half], res[:])
 
-        for f in range(2):
-            first = kept([P, T], F32, "first%d" % f)
-            nc.vector.tensor_tensor(first[:], y[f][:].indirect(pos_t[0][:]), gt[:, 0, :], MULT)
-            second = [kept([P, half], F32, "second%d_%d" % (f, b)) for b in range(2)]
-            for b in range(2):
-                lst = pos_t[1][:, b * half // 16 : (b + 1) * half // 16]
-                nc.vector.tensor_tensor(second[b][:], y[f][:].indirect(lst), gt[:, 1, b * half : (b + 1) * half], MULT)
-            for b in range(2):
-                res = kept([P, half], F32, "res%d_%d" % (f, b))
-                if f == 0:
-                    add_on_tensor(first[:, b * half : (b + 1) * half], second[b][:], res, b)
-                else:
-                    add_on_vector(first[:, b * half : (b + 1) * half], second[b][:], res)
-                queue = nc.scalar if f == 0 else nc.sync
-                queue.dma_start(out[f * P : (f + 1) * P, b * half : (b + 1) * half], res[:])
+        first = kept([P, T], F32, "first")
+        nc.vector.tensor_tensor(first[:], y[1][:].indirect(pos_t[0][:]), gt[:, 0, :], MULT)
+        second = [kept([P, half], F32, "second%d" % b) for b in range(2)]
+        for b in range(2):
+            nc.vector.tensor_tensor(second[b][:], y[1][:].indirect(tokens(1, b)), gt[:, 1, b * half : (b + 1) * half], MULT)
+        for b in range(2):
+            res = kept([P, half], F32, "res1_%d" % b)
+            nc.vector.tensor_tensor(res[:], first[:, b * half : (b + 1) * half], second[b][:], ADD)
+            nc.sync.dma_start(out[P : 2 * P, b * half : (b + 1) * half], res[:])

@@ -61,14 +61,13 @@ def tile_moe_elr_silu_kernel(tc, x_words, x_scales, w_words, w_scales, wa, wb_wo
         ident = kept([P, P], F32, "ident")
         gate_rows = kept([P, P], F32, "gate_rows")
         gate_cols = kept([P, 8], F32, "gate_cols")
-        warm = keep.tile([P, 8], F32, name="warm")
-        warm2 = keep.tile([P, 8], F32, name="warm2")
+        zeros = kept([P, P], F32, "zeros")
 
         nc.gpsimd.memset(wbst[:].bitcast(I32), 0)
         nc.gpsimd.memset(wst[:].bitcast(I32), 0)
-        nc.vector.memset(warm[:], 0.0)
+        nc.vector.memset(zeros[:], 0.0)
+        nc.scalar.activation(gate_rows[:], zeros[:], SILU)
         make_identity(nc, ident[:])
-        nc.gpsimd.memset(gate_rows[:], 0.0)
 
         def load_wa(dst, e, c0, c1):
             nc.sync.dma_start(dst[:], wa[e].rearrange("(p j) i -> p j i", j=4)[:, :, c0:c1])
@@ -85,7 +84,6 @@ def tile_moe_elr_silu_kernel(tc, x_words, x_scales, w_words, w_scales, wa, wb_wo
                 wbst[32 * q : 32 * q + 16].bitcast(I32),
                 wb_scales[:, 0, 4 * q : 4 * q + 4, :].bitcast(I32),
             )
-        nc.scalar.activation(warm2[:], warm[:], SILU)
         for e in range(E - 1):
             load_wa(raw[e], e, 0, H)
         load_wa(raw_last[0], 3, 0, H // 2)
@@ -152,19 +150,6 @@ def tile_moe_elr_silu_kernel(tc, x_words, x_scales, w_words, w_scales, wa, wb_wo
                         stop=True,
                     )
 
-        def keep_clock(e, passes):
-            spare = psum.tile([P, 2, C], F32, name="ya")
-            for t in range(passes):
-                nc.tensor.matmul_mx(
-                    out=spare[:, t % 2, :],
-                    lhsT=waq[:, e, t * P : (t + 1) * P].bitcast(FP8X4),
-                    lhsT_scale=was[:, e, t * P : (t + 1) * P],
-                    rhs=gw[e][:].bitcast(FP8X4),
-                    rhs_scale=gs[e][:],
-                    start=True,
-                    stop=True,
-                )
-
         def silu(e):
             for a in range(2):
                 nc.scalar.activation(hb[e][:, a * P : (a + 1) * P, :], banks[e, a][:].rearrange("p t s -> p s t"), SILU)
@@ -213,18 +198,15 @@ def tile_moe_elr_silu_kernel(tc, x_words, x_scales, w_words, w_scales, wa, wb_wo
         cast_pair(0, raw[0], 0, P, VECTOR_M[0])
         quant_wa(0)
         first_layer(0)
-        keep_clock(0, 3)
         gather(3)
         cast_pair(1, raw[1], 0, P, VECTOR_M[1])
         silu(0)
         quant_wa(1)
         first_layer(1)
-        keep_clock(1, 2)
         cast_pair(2, raw[2], 0, P, VECTOR_M[2])
         silu(1)
         quant_wa(2)
         first_layer(2)
-        keep_clock(2, 2)
         cast_pair(3, raw_last[0], 0, HALF, VECTOR_M[3])
         quant_wa_half(3, 0)
         cast_pair(3, raw_last[1], HALF, HALF, VECTOR_M[4])
@@ -244,40 +226,48 @@ def tile_moe_elr_silu_kernel(tc, x_words, x_scales, w_words, w_scales, wa, wb_wo
         results("yc", 1, 0, 4, nc.scalar.copy)
         results("yd", 1, 4, 8, nc.scalar.copy)
 
-        half = T // 2
         turned_gate = psum.tile([P, P], F32, name="ya")
         nc.tensor.transpose(turned_gate[:], gate_rows[:], ident[:])
         nc.scalar.copy(gate_cols[:], turned_gate[:, 0:8])
 
-        def tokens(r, b):
-            return pos_t[r][:, b * half // 16 : (b + 1) * half // 16]
+        def tokens(r, k0, k1):
+            return pos_t[r][:, k0 * P // 16 : k1 * P // 16]
 
-        for b in range(2):
-            picked = [kept([P, half], F32, "picked%d_%d" % (r, b)) for r in range(2)]
-            turned = psum.tile([P, 2, 2, P], F32, name="h%d" % (2 * b))
-            scaled = kept([P, 2, 2, P], F32, "scaled%d" % b)
-            back = psum.tile([P, 2, P], F32, name="h%d" % (2 * b + 1))
-            res = kept([P, half], F32, "res0_%d" % b)
-            for r in range(2):
-                nc.vector.tensor_copy(picked[r][:], y[0][:].indirect(tokens(r, b)))
-                for k in range(2):
-                    nc.tensor.transpose(turned[:, r, k, :], picked[r][:, k * P : (k + 1) * P], ident[:])
-            for r in range(2):
-                for k in range(2):
-                    col = 4 * r + 2 * b + k
-                    nc.scalar.activation(scaled[:, r, k, :], turned[:, r, k, :], COPY, scale=gate_cols[:, col : col + 1])
-            for k in range(2):
-                for r in range(2):
-                    nc.tensor.matmul(back[:, k, :], scaled[:, r, k, :], ident[:], start=r == 0, stop=r == 1, is_transpose=True)
+        def turn_back(f, k0, k1, parts, name):
+            n = k1 - k0
+            back = psum.tile([P, n, P], F32, name=name)
+            for k in range(n):
+                for r, part in enumerate(parts):
+                    nc.tensor.matmul(back[:, k, :], part[:, k, :], ident[:], start=r == 0, stop=r == len(parts) - 1, is_transpose=True)
+            res = kept([P, n * P], F32, "res%d_%d" % (f, k0))
             nc.scalar.copy(res[:], back[:].rearrange("p k t -> p (k t)"))
-            nc.scalar.dma_start(out[0:P, b * half : (b + 1) * half], res[:])
+            nc.scalar.dma_start(out[f * P : (f + 1) * P, k0 * P : k1 * P], res[:])
 
-        first = kept([P, T], F32, "first")
-        nc.vector.tensor_tensor(first[:], y[1][:].indirect(pos_t[0][:]), gt[:, 0, :], MULT)
-        second = [kept([P, half], F32, "second%d" % b) for b in range(2)]
+        def combine_plain(f, k0, k1, names):
+            n = k1 - k0
+            scaled = [kept([P, n, P], F32, "scaled%d_%d_%d" % (r, f, k0)) for r in range(2)]
+            for r in range(2):
+                picked = kept([P, n * P], F32, "picked%d_%d_%d" % (r, f, k0))
+                nc.vector.tensor_copy(picked[:], y[f][:].indirect(tokens(r, k0, k1)))
+                turned = psum.tile([P, n, P], F32, name=names[r])
+                for k in range(n):
+                    nc.tensor.transpose(turned[:, k, :], picked[:, k * P : (k + 1) * P], ident[:])
+                for k in range(n):
+                    col = 4 * r + k0 + k
+                    nc.scalar.activation(scaled[r][:, k, :], turned[:, k, :], COPY, scale=gate_cols[:, col : col + 1])
+            turn_back(f, k0, k1, scaled, names[2])
+
+        def gated(f, r, k0, k1):
+            part = kept([P, (k1 - k0) * P], F32, "gated%d_%d_%d" % (r, f, k0))
+            nc.vector.tensor_tensor(part[:], y[f][:].indirect(tokens(r, k0, k1)), gt[:, r, k0 * P : k1 * P], MULT)
+            return part
+
+        combine_plain(0, 0, 2, ("h0", "h1", "ya"))
+        combine_plain(0, 2, 4, ("h2", "h3", "yb"))
+
+        first = gated(1, 0, 0, 4)
+        second = [gated(1, 1, 2 * b, 2 * b + 2) for b in range(2)]
         for b in range(2):
-            nc.vector.tensor_tensor(second[b][:], y[1][:].indirect(tokens(1, b)), gt[:, 1, b * half : (b + 1) * half], MULT)
-        for b in range(2):
-            res = kept([P, half], F32, "res1_%d" % b)
-            nc.vector.tensor_tensor(res[:], first[:, b * half : (b + 1) * half], second[b][:], ADD)
-            nc.sync.dma_start(out[P : 2 * P, b * half : (b + 1) * half], res[:])
+            res = kept([P, 2 * P], F32, "res1_%d" % b)
+            nc.vector.tensor_tensor(res[:], first[:, 2 * b * P : 2 * (b + 1) * P], second[b][:], ADD)
+            nc.sync.dma_start(out[P : 2 * P, 2 * b * P : 2 * (b + 1) * P], res[:])

@@ -223,8 +223,8 @@ def tile_moe_elr_silu_kernel(tc, x_words, x_scales, w_words, w_scales, wa, wb_wo
         results("yb", 0, 4, 6, nc.vector.tensor_copy)
         results("yc", 0, 6, 7, nc.scalar.copy)
         results("yd", 0, 7, 8, nc.scalar.copy)
-        results("yc", 1, 0, 4, nc.scalar.copy)
-        results("yd", 1, 4, 8, nc.scalar.copy)
+        results("h0", 1, 0, 4, nc.scalar.copy)
+        results("h1", 1, 4, 8, nc.scalar.copy)
 
         turned_gate = psum.tile([P, P], F32, name="ya")
         nc.tensor.transpose(turned_gate[:], gate_rows[:], ident[:])
@@ -262,8 +262,8 @@ def tile_moe_elr_silu_kernel(tc, x_words, x_scales, w_words, w_scales, wa, wb_wo
             nc.vector.tensor_tensor(part[:], y[f][:].indirect(tokens(r, k0, k1)), gt[:, r, k0 * P : k1 * P], MULT)
             return part
 
-        combine_plain(0, 0, 2, ("h0", "h1", "ya"))
-        combine_plain(0, 2, 4, ("h2", "h3", "yb"))
+        combine_plain(0, 0, 2, ("h2", "h3", "ya"))
+        combine_plain(0, 2, 4, ("yc", "yd", "yb"))
 
         first = gated(1, 0, 0, 4)
         second = [gated(1, 1, 2 * b, 2 * b + 2) for b in range(2)]

@@ -152,7 +152,11 @@ def tile_moe_elr_silu_kernel(tc, x_words, x_scales, w_words, w_scales, wa, wb_wo
 
         def silu(e):
             for a in range(2):
-                nc.scalar.activation(hb[e][:, a * P : (a + 1) * P, :], banks[e, a][:].rearrange("p t s -> p s t"), SILU)
+                nc.scalar.activation(
+                    hb[e][:, a * P : (a + 1) * P, :].rearrange("p (s v) t -> p s t v", v=2),
+                    banks[e, a][:].rearrange("p t (s v) -> p s t v", v=2),
+                    SILU,
+                )
 
         def quant_h(e, s0, s1):
             nc.vector.quantize_mx(

@@ -22,7 +22,8 @@ ADD = mybir.AluOpType.add
 P = 128
 S = E * C
 HALF = P // 2
-VECTOR_M = (44, 52, 52, 60, 60)
+RAW = 16 * H
+VECTOR_M = (0, 104, 208, 176)
 
 
 def tile_moe_elr_silu_kernel(tc, x_words, x_scales, w_words, w_scales, wa, wb_words, wb_scales, gate, offs, pos1, pos2, out):
@@ -42,10 +43,9 @@ def tile_moe_elr_silu_kernel(tc, x_words, x_scales, w_words, w_scales, wa, wb_wo
         pos_t = [keep.tile([P, T // 16], U16, name="pos%d" % r) for r in range(2)]
         xw = kept([P, T], I32, "xw")
         xs = kept([P, T], U8, "xs")
-        raw = [placed([P, 4, H], F32, "raw0", 0)] + [kept([P, 4, H], F32, "raw%d" % e) for e in range(1, E - 1)]
-        raw_last = [kept([P, 4, H // 2], F32, "raw_last%d" % u) for u in range(2)]
-        gw = [kept([P, C], U32, "gw%d" % e) for e in range(E - 1)] + [placed([P, C], U32, "gw3", 0)]
-        gs = [kept([P, C], U8, "gs%d" % e) for e in range(E - 1)] + [placed([P, C], U8, "gs3", 4 * C)]
+        raw = [placed([P, 4, H], F32, "raw%d" % e, e * RAW) for e in range(E)]
+        gw = [kept([P, C], U32, "gw%d" % e) for e in range(E)]
+        gs = [kept([P, C], U8, "gs%d" % e) for e in range(E)]
         wab = [kept([P, 4, P, 4], BF16, "wab%d" % e) for e in range(E)]
         waq = kept([P, E, H], U32, "waq")
         was = kept([P, E, H], U8, "was")
@@ -54,8 +54,8 @@ def tile_moe_elr_silu_kernel(tc, x_words, x_scales, w_words, w_scales, wa, wb_wo
         wbt = kept([P, E, N], I32, "wbt")
         wbst = kept([P, N], U8, "wbst")
         gt = kept([P, 2, T], F32, "gt")
-        hb = [kept([P, C, 4], BF16, "hb%d" % e) for e in range(E)]
-        hq = [kept([P, C], U32, "hq%d" % e) for e in range(E)]
+        hb = [placed([P, C, 4], BF16, "hb%d" % e, (e + 1) * RAW) if e in (0, 2) else kept([P, C, 4], BF16, "hb%d" % e) for e in range(E)]
+        hq = [placed([P, C], U32, "hq%d" % e, 3 * RAW + 8 * C + 4 * C * e) for e in range(2)] + [kept([P, C], U32, "hq%d" % e) for e in range(2, E)]
         hs = kept([P, S], U8, "hs")
         y = [kept([P, S], F32, "y%d" % f) for f in range(2)]
         ident = kept([P, P], F32, "ident")
@@ -63,31 +63,29 @@ def tile_moe_elr_silu_kernel(tc, x_words, x_scales, w_words, w_scales, wa, wb_wo
         gate_cols = kept([P, 8], F32, "gate_cols")
         zeros = kept([P, P], F32, "zeros")
 
+        nc.gpsimd.memset(xs[:].bitcast(I32), 0)
         nc.gpsimd.memset(wbst[:].bitcast(I32), 0)
         nc.gpsimd.memset(wst[:].bitcast(I32), 0)
         nc.vector.memset(zeros[:], 0.0)
         nc.scalar.activation(gate_rows[:], zeros[:], SILU)
         make_identity(nc, ident[:])
 
-        def load_wa(dst, e, c0, c1):
-            nc.sync.dma_start(dst[:], wa[e].rearrange("(p j) i -> p j i", j=4)[:, :, c0:c1])
+        def load_wa(e):
+            nc.sync.dma_start(raw[e][:], wa[e].rearrange("(p j) i -> p j i", j=4))
 
-        nc.sync.dma_start(offs_t[:], offs)
         nc.sync.dma_start(xw[:], x_words[0].rearrange("p t d -> p (t d)").bitcast(I32))
+        nc.sync.dma_start(offs_t[:], offs)
         for q in range(4):
-            nc.sync.dma_start(
-                xs[32 * q : 32 * q + 32].bitcast(I32),
-                x_scales[0, 4 * q : 4 * q + 4, :].bitcast(I32).unsqueeze(0).broadcast_to([8, 4, T // 4]),
-            )
+            if q == 2:
+                load_wa(0)
+            nc.sync.dma_start(xs[32 * q : 32 * q + 4].bitcast(I32), x_scales[0, 4 * q : 4 * q + 4, :].bitcast(I32))
         for q in range(4):
             nc.gpsimd.dma_start(
                 wbst[32 * q : 32 * q + 16].bitcast(I32),
                 wb_scales[:, 0, 4 * q : 4 * q + 4, :].bitcast(I32),
             )
-        for e in range(E - 1):
-            load_wa(raw[e], e, 0, H)
-        load_wa(raw_last[0], 3, 0, H // 2)
-        load_wa(raw_last[1], 3, H // 2, H)
+        for e in range(1, E):
+            load_wa(e)
         for q in range(4):
             nc.sync.dma_start(
                 wst[32 * q : 32 * q + 4].bitcast(I32),
@@ -105,32 +103,31 @@ def tile_moe_elr_silu_kernel(tc, x_words, x_scales, w_words, w_scales, wa, wb_wo
             nc.vector.tensor_copy(gw[e][:], xw[:].bitcast(U32).indirect(lst))
             nc.vector.tensor_copy(gs[e][:], xs[:].indirect(lst))
 
-        def cast(engine_copy, e, src, base, m0, m1):
+        def cast(engine_copy, e, u, m0, m1):
             if m1 > m0:
                 engine_copy(
-                    wab[e][:, :, m0:m1, :].rearrange("p t m j -> p m j t"),
-                    src[:, :, 4 * (m0 - base) : 4 * (m1 - base)].rearrange("p j (m t) -> p m j t", t=4),
+                    wab[e][:, 2 * u : 2 * u + 2, m0:m1, :].rearrange("p t m j -> p m j t"),
+                    raw[e][:, :, 4 * m0 : 4 * m1].rearrange("p j (m t) -> p m j t", t=4)[:, :, :, 2 * u : 2 * u + 2],
                 )
 
-        def cast_pair(e, src, base, width, share):
-            cast(nc.vector.tensor_copy, e, src, base, base, base + share)
-            cast(nc.scalar.copy, e, src, base, base + share, base + width)
-
-        def quant_wa(e):
+        def quant_wa(e, u):
+            cols = slice(2 * u * P, 2 * (u + 1) * P)
             nc.vector.quantize_mx(
-                out=waq[:, e, :].bitcast(FP8X4),
-                scales=was[:, e, :],
-                in_=wab[e][:].rearrange("p t m j -> p (t m j)"),
+                out=waq[:, e, cols].bitcast(FP8X4),
+                scales=was[:, e, cols],
+                in_=wab[e][:, 2 * u : 2 * u + 2].rearrange("p t m j -> p (t m j)"),
             )
 
-        def quant_wa_half(e, u):
-            for t in range(4):
-                cols = slice(t * P + u * HALF, t * P + (u + 1) * HALF)
-                nc.vector.quantize_mx(
-                    out=waq[:, e, cols].bitcast(FP8X4),
-                    scales=was[:, e, cols],
-                    in_=wab[e][:, t, u * HALF : (u + 1) * HALF, :].rearrange("p m j -> p (m j)"),
-                )
+        def cast_wa(e):
+            share = VECTOR_M[e]
+            cast(nc.vector.tensor_copy, e, 0, 0, min(share, P))
+            cast(nc.vector.tensor_copy, e, 1, 0, share - P)
+            cast(nc.scalar.copy, e, 1, max(share - P, 0), P)
+            cast(nc.scalar.copy, e, 0, share, P)
+
+        def quant_both(e):
+            for u in (0, 1) if VECTOR_M[e] >= P else (1, 0):
+                quant_wa(e, u)
 
         banks = {}
 
@@ -197,26 +194,14 @@ def tile_moe_elr_silu_kernel(tc, x_words, x_scales, w_words, w_scales, wa, wb_wo
                 adapter(b // 2, f, b % 2, acc)
             engine_copy(y[f][:, b0 * P : b1 * P], bank[:])
 
-        for e in range(E - 1):
+        for e in range(E):
             gather(e)
-        cast_pair(0, raw[0], 0, P, VECTOR_M[0])
-        quant_wa(0)
-        first_layer(0)
-        gather(3)
-        cast_pair(1, raw[1], 0, P, VECTOR_M[1])
-        silu(0)
-        quant_wa(1)
-        first_layer(1)
-        cast_pair(2, raw[2], 0, P, VECTOR_M[2])
-        silu(1)
-        quant_wa(2)
-        first_layer(2)
-        cast_pair(3, raw_last[0], 0, HALF, VECTOR_M[3])
-        quant_wa_half(3, 0)
-        cast_pair(3, raw_last[1], HALF, HALF, VECTOR_M[4])
-        quant_wa_half(3, 1)
-        silu(2)
-        first_layer(3)
+        for e in range(E):
+            cast_wa(e)
+            if e > 0:
+                silu(e - 1)
+            quant_both(e)
+            first_layer(e)
         silu(3)
         quant_h(0, 0, C)
         quant_h(1, 0, C)

@@ -22,8 +22,9 @@ ADD = mybir.AluOpType.add
 P = 128
 S = E * C
 HALF = P // 2
+WINDOW = 704
 RAW = 16 * H
-VECTOR_M = (0, 104, 208, 176)
+VECTOR_M = (0, 104, 240, 176)
 
 
 def tile_moe_elr_silu_kernel(tc, x_words, x_scales, w_words, w_scales, wa, wb_words, wb_scales, gate, offs, pos1, pos2, out):
@@ -41,11 +42,11 @@ def tile_moe_elr_silu_kernel(tc, x_words, x_scales, w_words, w_scales, wa, wb_wo
 
         offs_t = keep.tile([P, S // 16], U16, name="offs_t")
         pos_t = [keep.tile([P, T // 16], U16, name="pos%d" % r) for r in range(2)]
-        xw = kept([P, T], I32, "xw")
-        xs = kept([P, T], U8, "xs")
+        xw = kept([P, WINDOW], I32, "xw")
+        xs = kept([P, WINDOW], U8, "xs")
         raw = [placed([P, 4, H], F32, "raw%d" % e, e * RAW) for e in range(E)]
-        gw = [kept([P, C], U32, "gw%d" % e) for e in range(E)]
-        gs = [kept([P, C], U8, "gs%d" % e) for e in range(E)]
+        gw = [kept([P, 2 * C], U32, "gw%d" % u) for u in range(2)]
+        gs = [kept([P, 2 * C], U8, "gs%d" % u) for u in range(2)]
         wab = [kept([P, 4, P, 4], BF16, "wab%d" % e) for e in range(E)]
         waq = kept([P, E, H], U32, "waq")
         was = kept([P, E, H], U8, "was")
@@ -54,12 +55,12 @@ def tile_moe_elr_silu_kernel(tc, x_words, x_scales, w_words, w_scales, wa, wb_wo
         wbt = kept([P, E, N], I32, "wbt")
         wbst = kept([P, N], U8, "wbst")
         gt = kept([P, 2, T], F32, "gt")
-        hb = [placed([P, C, 4], BF16, "hb%d" % e, (e + 1) * RAW) if e in (0, 2) else kept([P, C, 4], BF16, "hb%d" % e) for e in range(E)]
+        hb = [placed([P, C, 4], BF16, "hb%d" % e, RAW if e == 0 else 4 * RAW) if e in (0, 2) else kept([P, C, 4], BF16, "hb%d" % e) for e in range(E)]
         hq = [placed([P, C], U32, "hq%d" % e, 3 * RAW + 8 * C + 4 * C * e) for e in range(2)] + [kept([P, C], U32, "hq%d" % e) for e in range(2, E)]
         hs = kept([P, S], U8, "hs")
         y = [kept([P, S], F32, "y%d" % f) for f in range(2)]
         ident = kept([P, P], F32, "ident")
-        gate_rows = kept([P, P], F32, "gate_rows")
+        gate_rows = placed([P, P], F32, "gate_rows", 4 * RAW)
         gate_cols = kept([P, 8], F32, "gate_cols")
         zeros = kept([P, P], F32, "zeros")
 
@@ -67,18 +68,19 @@ def tile_moe_elr_silu_kernel(tc, x_words, x_scales, w_words, w_scales, wa, wb_wo
         nc.gpsimd.memset(wbst[:].bitcast(I32), 0)
         nc.gpsimd.memset(wst[:].bitcast(I32), 0)
         nc.vector.memset(zeros[:], 0.0)
+        nc.vector.memset(xw[:, T:WINDOW], 0)
         nc.scalar.activation(gate_rows[:], zeros[:], SILU)
         make_identity(nc, ident[:])
 
         def load_wa(e):
             nc.sync.dma_start(raw[e][:], wa[e].rearrange("(p j) i -> p j i", j=4))
 
-        nc.sync.dma_start(xw[:], x_words[0].rearrange("p t d -> p (t d)").bitcast(I32))
+        nc.sync.dma_start(xw[:, 0:T], x_words[0].rearrange("p t d -> p (t d)").bitcast(I32))
         nc.sync.dma_start(offs_t[:], offs)
         for q in range(4):
             if q == 2:
                 load_wa(0)
-            nc.sync.dma_start(xs[32 * q : 32 * q + 4].bitcast(I32), x_scales[0, 4 * q : 4 * q + 4, :].bitcast(I32))
+            nc.sync.dma_start(xs[32 * q : 32 * q + 4, 0:T].bitcast(I32), x_scales[0, 4 * q : 4 * q + 4, :].bitcast(I32))
         for q in range(4):
             nc.gpsimd.dma_start(
                 wbst[32 * q : 32 * q + 16].bitcast(I32),
@@ -86,6 +88,7 @@ def tile_moe_elr_silu_kernel(tc, x_words, x_scales, w_words, w_scales, wa, wb_wo
             )
         for e in range(1, E):
             load_wa(e)
+        nc.sync.dma_start(gate_rows[0:8], gate[:, 0, :].rearrange("r (k c) -> r k c", c=P))
         for q in range(4):
             nc.sync.dma_start(
                 wst[32 * q : 32 * q + 4].bitcast(I32),
@@ -95,39 +98,44 @@ def tile_moe_elr_silu_kernel(tc, x_words, x_scales, w_words, w_scales, wa, wb_wo
         nc.sync.dma_start(wt[:].bitcast(I32), w_words[:, 0].bitcast(I32).rearrange("e p b -> p e b"))
         nc.sync.dma_start(pos_t[0][:], pos1)
         nc.sync.dma_start(pos_t[1][:], pos2)
-        nc.sync.dma_start(gate_rows[0:8], gate[:, 0, :].rearrange("r (k c) -> r k c", c=P))
         nc.sync.dma_start(gt[:], gate.rearrange("r p t -> p r t"))
 
         def gather(e):
-            lst = offs_t[:, e * C // 16 : (e + 1) * C // 16]
+            lst = offs_t[:, e * 2 * C // 16 : (e + 1) * 2 * C // 16]
             nc.vector.tensor_copy(gw[e][:], xw[:].bitcast(U32).indirect(lst))
             nc.vector.tensor_copy(gs[e][:], xs[:].indirect(lst))
 
-        def cast(engine_copy, e, u, m0, m1):
+        def cast(engine_copy, e, t0, t1, m0, m1):
             if m1 > m0:
                 engine_copy(
-                    wab[e][:, 2 * u : 2 * u + 2, m0:m1, :].rearrange("p t m j -> p m j t"),
-                    raw[e][:, :, 4 * m0 : 4 * m1].rearrange("p j (m t) -> p m j t", t=4)[:, :, :, 2 * u : 2 * u + 2],
+                    wab[e][:, t0:t1, m0:m1, :].rearrange("p t m j -> p m j t"),
+                    raw[e][:, :, 4 * m0 : 4 * m1].rearrange("p j (m t) -> p m j t", t=4)[:, :, :, t0:t1],
                 )
 
-        def quant_wa(e, u):
-            cols = slice(2 * u * P, 2 * (u + 1) * P)
+        def quant_wa(e, t0, t1):
             nc.vector.quantize_mx(
-                out=waq[:, e, cols].bitcast(FP8X4),
-                scales=was[:, e, cols],
-                in_=wab[e][:, 2 * u : 2 * u + 2].rearrange("p t m j -> p (t m j)"),
+                out=waq[:, e, t0 * P : t1 * P].bitcast(FP8X4),
+                scales=was[:, e, t0 * P : t1 * P],
+                in_=wab[e][:, t0:t1].rearrange("p t m j -> p (t m j)"),
             )
 
         def cast_wa(e):
             share = VECTOR_M[e]
-            cast(nc.vector.tensor_copy, e, 0, 0, min(share, P))
-            cast(nc.vector.tensor_copy, e, 1, 0, share - P)
-            cast(nc.scalar.copy, e, 1, max(share - P, 0), P)
-            cast(nc.scalar.copy, e, 0, share, P)
+            if e in ():
+                cast(nc.vector.tensor_copy, e, 0, 4, 0, share // 2)
+                cast(nc.scalar.copy, e, 0, 4, share // 2, P)
+            else:
+                cast(nc.vector.tensor_copy, e, 0, 2, 0, min(share, P))
+                cast(nc.vector.tensor_copy, e, 2, 4, 0, share - P)
+                cast(nc.scalar.copy, e, 2, 4, max(share - P, 0), P)
+                cast(nc.scalar.copy, e, 0, 2, share, P)
 
         def quant_both(e):
-            for u in (0, 1) if VECTOR_M[e] >= P else (1, 0):
-                quant_wa(e, u)
+            if e in ():
+                quant_wa(e, 0, 4)
+            else:
+                for u in (0, 1) if VECTOR_M[e] >= P else (1, 0):
+                    quant_wa(e, 2 * u, 2 * u + 2)
 
         banks = {}
 
@@ -141,8 +149,8 @@ def tile_moe_elr_silu_kernel(tc, x_words, x_scales, w_words, w_scales, wa, wb_wo
                         out=bank[:, t, :],
                         lhsT=waq[:, e, t * P : (t + 1) * P].bitcast(FP8X4),
                         lhsT_scale=was[:, e, t * P : (t + 1) * P],
-                        rhs=gw[e][:, cols].bitcast(FP8X4),
-                        rhs_scale=gs[e][:, cols],
+                        rhs=gw[e // 2][:, (2 * (e % 2) + a) * P : (2 * (e % 2) + a + 1) * P].bitcast(FP8X4),
+                        rhs_scale=gs[e // 2][:, (2 * (e % 2) + a) * P : (2 * (e % 2) + a + 1) * P],
                         start=True,
                         stop=True,
                     )
@@ -168,8 +176,8 @@ def tile_moe_elr_silu_kernel(tc, x_words, x_scales, w_words, w_scales, wa, wb_wo
                 out=acc,
                 lhsT=wt[:, e, 2 * f * P : 2 * (f + 1) * P].bitcast(FP4X4),
                 lhsT_scale=wst[:, e, f * P : (f + 1) * P],
-                rhs=gw[e][:, cols].bitcast(FP8X4),
-                rhs_scale=gs[e][:, cols],
+                rhs=gw[e // 2][:, (2 * (e % 2) + a) * P : (2 * (e % 2) + a + 1) * P].bitcast(FP8X4),
+                rhs_scale=gs[e // 2][:, (2 * (e % 2) + a) * P : (2 * (e % 2) + a + 1) * P],
                 start=True,
                 stop=False,
             )
@@ -194,10 +202,14 @@ def tile_moe_elr_silu_kernel(tc, x_words, x_scales, w_words, w_scales, wa, wb_wo
                 adapter(b // 2, f, b % 2, acc)
             engine_copy(y[f][:, b0 * P : b1 * P], bank[:])
 
-        for e in range(E):
+        for e in range(2):
             gather(e)
         for e in range(E):
             cast_wa(e)
+            if e == 3:
+                turned_gate = psum.tile([P, P], F32, name="ya")
+                nc.tensor.transpose(turned_gate[:], gate_rows[:], ident[:])
+                nc.scalar.copy(gate_cols[:], turned_gate[:, 0:8])
             if e > 0:
                 silu(e - 1)
             quant_both(e)
@@ -215,44 +227,41 @@ def tile_moe_elr_silu_kernel(tc, x_words, x_scales, w_words, w_scales, wa, wb_wo
         results("h0", 1, 0, 4, nc.scalar.copy)
         results("h1", 1, 4, 8, nc.scalar.copy)
 
-        turned_gate = psum.tile([P, P], F32, name="ya")
-        nc.tensor.transpose(turned_gate[:], gate_rows[:], ident[:])
-        nc.scalar.copy(gate_cols[:], turned_gate[:, 0:8])
 
         def tokens(r, k0, k1):
             return pos_t[r][:, k0 * P // 16 : k1 * P // 16]
 
-        def turn_back(f, k0, k1, parts, name):
-            n = k1 - k0
-            back = psum.tile([P, n, P], F32, name=name)
-            for k in range(n):
-                for r, part in enumerate(parts):
-                    nc.tensor.matmul(back[:, k, :], part[:, k, :], ident[:], start=r == 0, stop=r == len(parts) - 1, is_transpose=True)
-            res = kept([P, n * P], F32, "res%d_%d" % (f, k0))
-            nc.scalar.copy(res[:], back[:].rearrange("p k t -> p (k t)"))
-            nc.scalar.dma_start(out[f * P : (f + 1) * P, k0 * P : k1 * P], res[:])
+        def turn(picked, k0, k1, name):
+            turned = psum.tile([P, k1 - k0, P], F32, name=name)
+            for k in range(k0, k1):
+                nc.tensor.transpose(turned[:, k - k0, :], picked[:, k * P : (k + 1) * P], ident[:])
+            return turned
 
-        def combine_plain(f, k0, k1, names):
-            n = k1 - k0
-            scaled = [kept([P, n, P], F32, "scaled%d_%d_%d" % (r, f, k0)) for r in range(2)]
-            for r in range(2):
-                picked = kept([P, n * P], F32, "picked%d_%d_%d" % (r, f, k0))
-                nc.vector.tensor_copy(picked[:], y[f][:].indirect(tokens(r, k0, k1)))
-                turned = psum.tile([P, n, P], F32, name=names[r])
-                for k in range(n):
-                    nc.tensor.transpose(turned[:, k, :], picked[:, k * P : (k + 1) * P], ident[:])
-                for k in range(n):
-                    col = 4 * r + k0 + k
-                    nc.scalar.activation(scaled[r][:, k, :], turned[:, k, :], COPY, scale=gate_cols[:, col : col + 1])
-            turn_back(f, k0, k1, scaled, names[2])
+        def scale(r, turned, k0, k1):
+            for k in range(k0, k1):
+                nc.scalar.activation(scaled[r][:, k, :], turned[:, k - k0, :], COPY, scale=gate_cols[:, 4 * r + k : 4 * r + k + 1])
 
         def gated(f, r, k0, k1):
             part = kept([P, (k1 - k0) * P], F32, "gated%d_%d_%d" % (r, f, k0))
             nc.vector.tensor_tensor(part[:], y[f][:].indirect(tokens(r, k0, k1)), gt[:, r, k0 * P : k1 * P], MULT)
             return part
 
-        combine_plain(0, 0, 2, ("h2", "h3", "ya"))
-        combine_plain(0, 2, 4, ("yc", "yd", "yb"))
+        picked = [kept([P, T], F32, "picked%d" % r) for r in range(2)]
+        scaled = [kept([P, 4, P], F32, "scaled%d" % r) for r in range(2)]
+        upper = kept([P, T], F32, "upper")
+        nc.vector.tensor_copy(picked[0][:], y[0][:].indirect(pos_t[0][:]))
+        for b in range(2):
+            nc.vector.tensor_copy(picked[1][:, 2 * b * P : 2 * (b + 1) * P], y[0][:].indirect(tokens(1, 2 * b, 2 * b + 2)))
+        back = [psum.tile([P, P], F32, name=name) for name in ("ya", "yb", "yd", "h0")]
+        for r, k0, name in ((0, 0, "h2"), (0, 2, "h3"), (1, 0, "yc"), (1, 2, "h1")):
+            scale(r, turn(picked[r], k0, k0 + 2, name), k0, k0 + 2)
+        for r, k0 in ((0, 0), (0, 2), (1, 0), (1, 2)):
+            for k in range(k0, k0 + 2):
+                nc.tensor.matmul(back[k][:], scaled[r][:, k, :], ident[:], start=r == 0, stop=r == 1, is_transpose=True)
+        for k in range(4):
+            nc.scalar.copy(upper[:, k * P : (k + 1) * P], back[k][:])
+        for b in range(2):
+            nc.scalar.dma_start(out[0:P, 2 * b * P : 2 * (b + 1) * P], upper[:, 2 * b * P : 2 * (b + 1) * P])
 
         first = gated(1, 0, 0, 4)
         second = [gated(1, 1, 2 * b, 2 * b + 2) for b in range(2)]

@@ -81,11 +81,6 @@ def tile_moe_elr_silu_kernel(tc, x_words, x_scales, w_words, w_scales, wa, wb_wo
             if q == 2:
                 load_wa(0)
             nc.sync.dma_start(xs[32 * q : 32 * q + 4, 0:T].bitcast(I32), x_scales[0, 4 * q : 4 * q + 4, :].bitcast(I32))
-        for q in range(4):
-            nc.gpsimd.dma_start(
-                wbst[32 * q : 32 * q + 16].bitcast(I32),
-                wb_scales[:, 0, 4 * q : 4 * q + 4, :].bitcast(I32),
-            )
         for e in range(1, E):
             load_wa(e)
         nc.sync.dma_start(gate_rows[0:8], gate[:, 0, :].rearrange("r (k c) -> r k c", c=P))
@@ -96,6 +91,11 @@ def tile_moe_elr_silu_kernel(tc, x_words, x_scales, w_words, w_scales, wa, wb_wo
             )
         nc.sync.dma_start(wbt[:], wb_words[:, 0].rearrange("e p n d -> p e (n d)").bitcast(I32))
         nc.sync.dma_start(wt[:].bitcast(I32), w_words[:, 0].bitcast(I32).rearrange("e p b -> p e b"))
+        for q in range(4):
+            nc.sync.dma_start(
+                wbst[32 * q : 32 * q + 16].bitcast(I32),
+                wb_scales[:, 0, 4 * q : 4 * q + 4, :].bitcast(I32),
+            )
         nc.sync.dma_start(pos_t[0][:], pos1)
         nc.sync.dma_start(pos_t[1][:], pos2)
         nc.sync.dma_start(gt[:], gate.rearrange("r p t -> p r t"))

@@ -24,7 +24,7 @@ S = E * C
 HALF = P // 2
 WINDOW = 704
 RAW = 16 * H
-VECTOR_M = (0, 104, 240, 176)
+VECTOR_M = (0, 128, 256, 180)
 
 
 def tile_moe_elr_silu_kernel(tc, x_words, x_scales, w_words, w_scales, wa, wb_words, wb_scales, gate, offs, pos1, pos2, out):
@@ -207,9 +207,8 @@ def tile_moe_elr_silu_kernel(tc, x_words, x_scales, w_words, w_scales, wa, wb_wo
         for e in range(E):
             cast_wa(e)
             if e == 3:
-                turned_gate = psum.tile([P, P], F32, name="ya")
+                turned_gate = psum.tile([P, P], F32, name="yd")
                 nc.tensor.transpose(turned_gate[:], gate_rows[:], ident[:])
-                nc.scalar.copy(gate_cols[:], turned_gate[:, 0:8])
             if e > 0:
                 silu(e - 1)
             quant_both(e)
@@ -217,6 +216,7 @@ def tile_moe_elr_silu_kernel(tc, x_words, x_scales, w_words, w_scales, wa, wb_wo
         silu(3)
         quant_h(0, 0, C)
         quant_h(1, 0, C)
+        nc.vector.tensor_copy(gate_cols[:], turned_gate[:, 0:8])
         quant_h(2, 0, C)
         quant_h(3, 0, P)
         quant_h(3, P, C)
@@ -249,14 +249,14 @@ def tile_moe_elr_silu_kernel(tc, x_words, x_scales, w_words, w_scales, wa, wb_wo
         picked = [kept([P, T], F32, "picked%d" % r) for r in range(2)]
         scaled = [kept([P, 4, P], F32, "scaled%d" % r) for r in range(2)]
         upper = kept([P, T], F32, "upper")
-        nc.vector.tensor_copy(picked[0][:], y[0][:].indirect(pos_t[0][:]))
-        for b in range(2):
-            nc.vector.tensor_copy(picked[1][:, 2 * b * P : 2 * (b + 1) * P], y[0][:].indirect(tokens(1, 2 * b, 2 * b + 2)))
+        for r in range(2):
+            nc.vector.tensor_copy(picked[r][:], y[0][:].indirect(pos_t[r][:]))
         back = [psum.tile([P, P], F32, name=name) for name in ("ya", "yb", "yd", "h0")]
-        for r, k0, name in ((0, 0, "h2"), (0, 2, "h3"), (1, 0, "yc"), (1, 2, "h1")):
-            scale(r, turn(picked[r], k0, k0 + 2, name), k0, k0 + 2)
-        for r, k0 in ((0, 0), (0, 2), (1, 0), (1, 2)):
-            for k in range(k0, k0 + 2):
+        for r, names in enumerate((("h2", "h3"), ("yc", "h1"))):
+            for b, name in enumerate(names):
+                scale(r, turn(picked[r], 2 * b, 2 * b + 2, name), 2 * b, 2 * b + 2)
+        for r in range(2):
+            for k in range(4):
                 nc.tensor.matmul(back[k][:], scaled[r][:, k, :], ident[:], start=r == 0, stop=r == 1, is_transpose=True)
         for k in range(4):
             nc.scalar.copy(upper[:, k * P : (k + 1) * P], back[k][:])

@@ -21,10 +21,11 @@ ADD = mybir.AluOpType.add
 
 P = 128
 S = E * C
-HALF = P // 2
+BLOCKS = S // P
 WINDOW = 704
 RAW = 16 * H
 VECTOR_M = (0, 128, 256, 180)
+GATHERS = ((0, 4), (4, 8))
 
 
 def tile_moe_elr_silu_kernel(tc, x_words, x_scales, w_words, w_scales, wa, wb_words, wb_scales, gate, offs, pos1, pos2, out):
@@ -45,8 +46,8 @@ def tile_moe_elr_silu_kernel(tc, x_words, x_scales, w_words, w_scales, wa, wb_wo
         xw = kept([P, WINDOW], I32, "xw")
         xs = kept([P, WINDOW], U8, "xs")
         raw = [placed([P, 4, H], F32, "raw%d" % e, e * RAW) for e in range(E)]
-        gw = [kept([P, 2 * C], U32, "gw%d" % u) for u in range(2)]
-        gs = [kept([P, 2 * C], U8, "gs%d" % u) for u in range(2)]
+        gw = [kept([P, (b1 - b0) * P], U32, "gw%d" % b0) for b0, b1 in GATHERS]
+        gs = [kept([P, (b1 - b0) * P], U8, "gs%d" % b0) for b0, b1 in GATHERS]
         wab = [kept([P, 4, P, 4], BF16, "wab%d" % e) for e in range(E)]
         waq = kept([P, E, H], U32, "waq")
         was = kept([P, E, H], U8, "was")
@@ -65,8 +66,8 @@ def tile_moe_elr_silu_kernel(tc, x_words, x_scales, w_words, w_scales, wa, wb_wo
         zeros = kept([P, P], F32, "zeros")
 
         nc.gpsimd.memset(xs[:].bitcast(I32), 0)
-        nc.gpsimd.memset(wbst[:].bitcast(I32), 0)
         nc.gpsimd.memset(wst[:].bitcast(I32), 0)
+        nc.gpsimd.memset(wbst[:].bitcast(I32), 0)
         nc.vector.memset(zeros[:], 0.0)
         nc.vector.memset(xw[:, T:WINDOW], 0)
         nc.scalar.activation(gate_rows[:], zeros[:], SILU)
@@ -89,8 +90,8 @@ def tile_moe_elr_silu_kernel(tc, x_words, x_scales, w_words, w_scales, wa, wb_wo
                 wst[32 * q : 32 * q + 4].bitcast(I32),
                 w_scales[:, 0, 4 * q : 4 * q + 4, :].bitcast(I32).rearrange("e r n -> r e n"),
             )
-        nc.sync.dma_start(wbt[:], wb_words[:, 0].rearrange("e p n d -> p e (n d)").bitcast(I32))
         nc.sync.dma_start(wt[:].bitcast(I32), w_words[:, 0].bitcast(I32).rearrange("e p b -> p e b"))
+        nc.sync.dma_start(wbt[:], wb_words[:, 0].rearrange("e p n d -> p e (n d)").bitcast(I32))
         for q in range(4):
             nc.sync.dma_start(
                 wbst[32 * q : 32 * q + 16].bitcast(I32),
@@ -100,133 +101,138 @@ def tile_moe_elr_silu_kernel(tc, x_words, x_scales, w_words, w_scales, wa, wb_wo
         nc.sync.dma_start(pos_t[1][:], pos2)
         nc.sync.dma_start(gt[:], gate.rearrange("r p t -> p r t"))
 
-        def gather(e):
-            lst = offs_t[:, e * 2 * C // 16 : (e + 1) * 2 * C // 16]
-            nc.vector.tensor_copy(gw[e][:], xw[:].bitcast(U32).indirect(lst))
-            nc.vector.tensor_copy(gs[e][:], xs[:].indirect(lst))
+        def gather(u):
+            b0, b1 = GATHERS[u]
+            lst = offs_t[:, b0 * P // 16 : b1 * P // 16]
+            nc.vector.tensor_copy(gw[u][:], xw[:].bitcast(U32).indirect(lst))
+            nc.vector.tensor_copy(gs[u][:], xs[:].indirect(lst))
 
-        def cast(engine_copy, e, t0, t1, m0, m1):
+        def tokens_of(b):
+            u = [b0 <= b < b1 for b0, b1 in GATHERS].index(True)
+            cols = slice((b - GATHERS[u][0]) * P, (b - GATHERS[u][0] + 1) * P)
+            return gw[u][:, cols].bitcast(FP8X4), gs[u][:, cols]
+
+        def cast(engine_copy, e, t0, m0, m1):
             if m1 > m0:
                 engine_copy(
-                    wab[e][:, t0:t1, m0:m1, :].rearrange("p t m j -> p m j t"),
-                    raw[e][:, :, 4 * m0 : 4 * m1].rearrange("p j (m t) -> p m j t", t=4)[:, :, :, t0:t1],
+                    wab[e][:, t0 : t0 + 2, m0:m1, :].rearrange("p t m j -> p m j t"),
+                    raw[e][:, :, 4 * m0 : 4 * m1].rearrange("p j (m t) -> p m j t", t=4)[:, :, :, t0 : t0 + 2],
                 )
-
-        def quant_wa(e, t0, t1):
-            nc.vector.quantize_mx(
-                out=waq[:, e, t0 * P : t1 * P].bitcast(FP8X4),
-                scales=was[:, e, t0 * P : t1 * P],
-                in_=wab[e][:, t0:t1].rearrange("p t m j -> p (t m j)"),
-            )
 
         def cast_wa(e):
             share = VECTOR_M[e]
-            if e in ():
-                cast(nc.vector.tensor_copy, e, 0, 4, 0, share // 2)
-                cast(nc.scalar.copy, e, 0, 4, share // 2, P)
-            else:
-                cast(nc.vector.tensor_copy, e, 0, 2, 0, min(share, P))
-                cast(nc.vector.tensor_copy, e, 2, 4, 0, share - P)
-                cast(nc.scalar.copy, e, 2, 4, max(share - P, 0), P)
-                cast(nc.scalar.copy, e, 0, 2, share, P)
+            cast(nc.vector.tensor_copy, e, 0, 0, min(share, P))
+            cast(nc.vector.tensor_copy, e, 2, 0, share - P)
+            cast(nc.scalar.copy, e, 2, max(share - P, 0), P)
+            cast(nc.scalar.copy, e, 0, share, P)
 
-        def quant_both(e):
-            if e in ():
-                quant_wa(e, 0, 4)
-            else:
-                for u in (0, 1) if VECTOR_M[e] >= P else (1, 0):
-                    quant_wa(e, 2 * u, 2 * u + 2)
-
-        banks = {}
-
-        def first_layer(e):
-            for a in range(2):
-                cols = slice(a * P, (a + 1) * P)
-                bank = psum.tile([P, 4, P], F32, name="h%d" % (2 * (e % 2) + a))
-                banks[e, a] = bank
-                for t in range(4):
-                    nc.tensor.matmul_mx(
-                        out=bank[:, t, :],
-                        lhsT=waq[:, e, t * P : (t + 1) * P].bitcast(FP8X4),
-                        lhsT_scale=was[:, e, t * P : (t + 1) * P],
-                        rhs=gw[e // 2][:, (2 * (e % 2) + a) * P : (2 * (e % 2) + a + 1) * P].bitcast(FP8X4),
-                        rhs_scale=gs[e // 2][:, (2 * (e % 2) + a) * P : (2 * (e % 2) + a + 1) * P],
-                        start=True,
-                        stop=True,
-                    )
-
-        def silu(e):
-            for a in range(2):
-                nc.scalar.activation(
-                    hb[e][:, a * P : (a + 1) * P, :].rearrange("p (s v) t -> p s t v", v=2),
-                    banks[e, a][:].rearrange("p t (s v) -> p s t v", v=2),
-                    SILU,
+        def quant_wa(e):
+            for t0 in (0, 2) if VECTOR_M[e] >= P else (2, 0):
+                nc.vector.quantize_mx(
+                    out=waq[:, e, t0 * P : (t0 + 2) * P].bitcast(FP8X4),
+                    scales=was[:, e, t0 * P : (t0 + 2) * P],
+                    in_=wab[e][:, t0 : t0 + 2].rearrange("p t m j -> p (t m j)"),
                 )
 
-        def quant_h(e, s0, s1):
+        h_banks = {}
+
+        def first_layer(b):
+            e = b // 2
+            words, scales = tokens_of(b)
+            h_banks[b] = psum.tile([P, 4, P], F32, name="h%d" % (b % 4))
+            for t in range(4):
+                nc.tensor.matmul_mx(
+                    out=h_banks[b][:, t, :],
+                    lhsT=waq[:, e, t * P : (t + 1) * P].bitcast(FP8X4),
+                    lhsT_scale=was[:, e, t * P : (t + 1) * P],
+                    rhs=words,
+                    rhs_scale=scales,
+                    start=True,
+                    stop=True,
+                )
+
+        def silu(b):
+            nc.scalar.activation(
+                hb[b // 2][:, b % 2 * P : (b % 2 + 1) * P, :].rearrange("p (s v) t -> p s t v", v=2),
+                h_banks[b][:].rearrange("p t (s v) -> p s t v", v=2),
+                SILU,
+            )
+
+        def quant_h(b0, b1):
+            e, s0, s1 = b0 // 2, b0 % 2 * P, (b1 - b0 + b0 % 2) * P
             nc.vector.quantize_mx(
                 out=hq[e][:, s0:s1].bitcast(FP8X4),
-                scales=hs[:, e * C + s0 : e * C + s1],
+                scales=hs[:, b0 * P : b1 * P],
                 in_=hb[e][:, s0:s1, :].rearrange("p s t -> p (s t)"),
             )
 
-        def frozen(e, f, a, acc):
-            cols = slice(a * P, (a + 1) * P)
+        def frozen(bank, f, b0, b, start):
+            words, scales = tokens_of(b)
             nc.tensor.matmul_mx(
-                out=acc,
-                lhsT=wt[:, e, 2 * f * P : 2 * (f + 1) * P].bitcast(FP4X4),
-                lhsT_scale=wst[:, e, f * P : (f + 1) * P],
-                rhs=gw[e // 2][:, (2 * (e % 2) + a) * P : (2 * (e % 2) + a + 1) * P].bitcast(FP8X4),
-                rhs_scale=gs[e // 2][:, (2 * (e % 2) + a) * P : (2 * (e % 2) + a + 1) * P],
-                start=True,
+                out=bank[:, (b - b0) * P : (b - b0 + 1) * P],
+                lhsT=wt[:, b // 2, 2 * f * P : 2 * (f + 1) * P].bitcast(FP4X4),
+                lhsT_scale=wst[:, b // 2, f * P : (f + 1) * P],
+                rhs=words,
+                rhs_scale=scales,
+                start=start,
                 stop=False,
             )
 
-        def adapter(e, f, a, acc):
-            cols = slice(a * P, (a + 1) * P)
+        def adapter(bank, f, b0, c0, c1, start, stop):
+            e = c0 // 2
             nc.tensor.matmul_mx(
-                out=acc,
+                out=bank[:, (c0 - b0) * P : (c1 - b0) * P],
                 lhsT=wbt[:, e, f * P : (f + 1) * P].bitcast(FP8X4),
                 lhsT_scale=wbst[4 * e :, f * P : (f + 1) * P],
-                rhs=hq[e][:, cols].bitcast(FP8X4),
-                rhs_scale=hs[:, e * C + a * P : e * C + (a + 1) * P],
-                start=False,
-                stop=True,
+                rhs=hq[e][:, (c0 - 2 * e) * P : (c1 - 2 * e) * P].bitcast(FP8X4),
+                rhs_scale=hs[:, c0 * P : c1 * P],
+                start=start,
+                stop=stop,
             )
 
-        def results(name, f, b0, b1, engine_copy):
+        def upper_rows(name, b0, b1, engine_copy):
             bank = psum.tile([P, (b1 - b0) * P], F32, name=name)
             for b in range(b0, b1):
-                acc = bank[:, (b - b0) * P : (b - b0 + 1) * P]
-                frozen(b // 2, f, b % 2, acc)
-                adapter(b // 2, f, b % 2, acc)
-            engine_copy(y[f][:, b0 * P : b1 * P], bank[:])
+                frozen(bank, 0, b0, b, b == b0)
+            for e in range(b0 // 2, (b1 + 1) // 2):
+                c0, c1 = max(b0, 2 * e), min(b1, 2 * e + 2)
+                adapter(bank, 0, b0, c0, c1, False, c1 == b1)
+            engine_copy(y[0][:, b0 * P : b1 * P], bank[:])
 
-        for e in range(2):
-            gather(e)
+        def lower_rows(name, b0):
+            bank = psum.tile([P, 4 * P], F32, name=name)
+            adapter(bank, 1, b0, b0, b0 + 2, True, False)
+            for b in range(b0, b0 + 4):
+                frozen(bank, 1, b0, b, False)
+            adapter(bank, 1, b0, b0 + 2, b0 + 4, False, True)
+            nc.scalar.copy(y[1][:, b0 * P : (b0 + 4) * P], bank[:])
+
+        gather(0)
+        gather(1)
         for e in range(E):
             cast_wa(e)
-            if e == 3:
+            if e == E - 1:
                 turned_gate = psum.tile([P, P], F32, name="yd")
                 nc.tensor.transpose(turned_gate[:], gate_rows[:], ident[:])
             if e > 0:
-                silu(e - 1)
-            quant_both(e)
-            first_layer(e)
-        silu(3)
-        quant_h(0, 0, C)
-        quant_h(1, 0, C)
+                silu(2 * e - 2)
+                silu(2 * e - 1)
+            quant_wa(e)
+            first_layer(2 * e)
+            first_layer(2 * e + 1)
+        silu(6)
+        silu(7)
+        quant_h(0, 2)
+        quant_h(2, 4)
         nc.vector.tensor_copy(gate_cols[:], turned_gate[:, 0:8])
-        quant_h(2, 0, C)
-        quant_h(3, 0, P)
-        quant_h(3, P, C)
-        results("ya", 0, 0, 4, nc.scalar.copy)
-        results("yb", 0, 4, 6, nc.vector.tensor_copy)
-        results("yc", 0, 6, 7, nc.scalar.copy)
-        results("yd", 0, 7, 8, nc.scalar.copy)
-        results("h0", 1, 0, 4, nc.scalar.copy)
-        results("h1", 1, 4, 8, nc.scalar.copy)
-
+        quant_h(4, 6)
+        quant_h(6, 7)
+        quant_h(7, 8)
+        upper_rows("ya", 0, 4, nc.scalar.copy)
+        upper_rows("yb", 4, 7, nc.vector.tensor_copy)
+        upper_rows("yc", 7, 8, nc.scalar.copy)
+        lower_rows("yd", 0)
+        lower_rows("h0", 4)
 
         def tokens(r, k0, k1):
             return pos_t[r][:, k0 * P // 16 : k1 * P // 16]
@@ -251,10 +257,10 @@ def tile_moe_elr_silu_kernel(tc, x_words, x_scales, w_words, w_scales, wa, wb_wo
         upper = kept([P, T], F32, "upper")
         for r in range(2):
             nc.vector.tensor_copy(picked[r][:], y[0][:].indirect(pos_t[r][:]))
-        back = [psum.tile([P, P], F32, name=name) for name in ("ya", "yb", "yd", "h0")]
         for r, names in enumerate((("h2", "h3"), ("yc", "h1"))):
             for b, name in enumerate(names):
                 scale(r, turn(picked[r], 2 * b, 2 * b + 2, name), 2 * b, 2 * b + 2)
+        back = [psum.tile([P, P], F32, name=name) for name in ("ya", "yb", "yd", "h0")]
         for r in range(2):
             for k in range(4):
                 nc.tensor.matmul(back[k][:], scaled[r][:, k, :], ident[:], start=r == 0, stop=r == 1, is_transpose=True)

@@ -21,10 +21,10 @@ ADD = mybir.AluOpType.add
 
 P = 128
 S = E * C
-BLOCKS = S // P
+HALF = T // 2
 WINDOW = 704
 RAW = 16 * H
-VECTOR_M = (0, 128, 256, 180)
+VECTOR_M = (0, 104, 256, 188)
 GATHERS = ((0, 4), (4, 8))
 
 
@@ -55,21 +55,27 @@ def tile_moe_elr_silu_kernel(tc, x_words, x_scales, w_words, w_scales, wa, wb_wo
         wst = kept([P, E, N], U8, "wst")
         wbt = kept([P, E, N], I32, "wbt")
         wbst = kept([P, N], U8, "wbst")
-        gt = kept([P, 2, T], F32, "gt")
+        gt = [kept([P, T], F32, "gt%d" % r) for r in range(2)]
         hb = [placed([P, C, 4], BF16, "hb%d" % e, RAW if e == 0 else 4 * RAW) if e in (0, 2) else kept([P, C, 4], BF16, "hb%d" % e) for e in range(E)]
         hq = [placed([P, C], U32, "hq%d" % e, 3 * RAW + 8 * C + 4 * C * e) for e in range(2)] + [kept([P, C], U32, "hq%d" % e) for e in range(2, E)]
         hs = kept([P, S], U8, "hs")
         y = [kept([P, S], F32, "y%d" % f) for f in range(2)]
         ident = kept([P, P], F32, "ident")
         gate_rows = placed([P, P], F32, "gate_rows", 4 * RAW)
-        gate_cols = kept([P, 8], F32, "gate_cols")
+        gate_cols = kept([P, 2], F32, "gate_cols")
         zeros = kept([P, P], F32, "zeros")
 
         nc.gpsimd.memset(xs[:].bitcast(I32), 0)
         nc.gpsimd.memset(wst[:].bitcast(I32), 0)
         nc.gpsimd.memset(wbst[:].bitcast(I32), 0)
-        nc.vector.memset(zeros[:], 0.0)
         nc.vector.memset(xw[:, T:WINDOW], 0)
+        nc.vector.memset(zeros[:], 0.0)
+
+        def load_x_scales(queue, q):
+            queue.dma_start(xs[32 * q : 32 * q + 4, 0:T].bitcast(I32), x_scales[0, 4 * q : 4 * q + 4, :].bitcast(I32))
+
+        load_x_scales(nc.scalar, 0)
+        load_x_scales(nc.scalar, 1)
         nc.scalar.activation(gate_rows[:], zeros[:], SILU)
         make_identity(nc, ident[:])
 
@@ -78,13 +84,12 @@ def tile_moe_elr_silu_kernel(tc, x_words, x_scales, w_words, w_scales, wa, wb_wo
 
         nc.sync.dma_start(xw[:, 0:T], x_words[0].rearrange("p t d -> p (t d)").bitcast(I32))
         nc.sync.dma_start(offs_t[:], offs)
-        for q in range(4):
-            if q == 2:
-                load_wa(0)
-            nc.sync.dma_start(xs[32 * q : 32 * q + 4, 0:T].bitcast(I32), x_scales[0, 4 * q : 4 * q + 4, :].bitcast(I32))
+        load_wa(0)
+        load_x_scales(nc.sync, 2)
+        load_x_scales(nc.sync, 3)
         for e in range(1, E):
             load_wa(e)
-        nc.sync.dma_start(gate_rows[0:8], gate[:, 0, :].rearrange("r (k c) -> r k c", c=P))
+        nc.sync.dma_start(gate_rows[0:2], gate[1, 0, HALF:T].rearrange("(k c) -> k c", c=P))
         for q in range(4):
             nc.sync.dma_start(
                 wst[32 * q : 32 * q + 4].bitcast(I32),
@@ -99,7 +104,8 @@ def tile_moe_elr_silu_kernel(tc, x_words, x_scales, w_words, w_scales, wa, wb_wo
             )
         nc.sync.dma_start(pos_t[0][:], pos1)
         nc.sync.dma_start(pos_t[1][:], pos2)
-        nc.sync.dma_start(gt[:], gate.rearrange("r p t -> p r t"))
+        nc.sync.dma_start(gt[0][:], gate[0])
+        nc.sync.dma_start(gt[1][:], gate[1])
 
         def gather(u):
             b0, b1 = GATHERS[u]
@@ -107,9 +113,9 @@ def tile_moe_elr_silu_kernel(tc, x_words, x_scales, w_words, w_scales, wa, wb_wo
             nc.vector.tensor_copy(gw[u][:], xw[:].bitcast(U32).indirect(lst))
             nc.vector.tensor_copy(gs[u][:], xs[:].indirect(lst))
 
-        def tokens_of(b):
-            u = [b0 <= b < b1 for b0, b1 in GATHERS].index(True)
-            cols = slice((b - GATHERS[u][0]) * P, (b - GATHERS[u][0] + 1) * P)
+        def tokens_of(c0, c1):
+            u = [b0 <= c0 < b1 for b0, b1 in GATHERS].index(True)
+            cols = slice((c0 - GATHERS[u][0]) * P, (c1 - GATHERS[u][0]) * P)
             return gw[u][:, cols].bitcast(FP8X4), gs[u][:, cols]
 
         def cast(engine_copy, e, t0, m0, m1):
@@ -138,9 +144,9 @@ def tile_moe_elr_silu_kernel(tc, x_words, x_scales, w_words, w_scales, wa, wb_wo
 
         def first_layer(b):
             e = b // 2
-            words, scales = tokens_of(b)
+            words, scales = tokens_of(b, b + 1)
             h_banks[b] = psum.tile([P, 4, P], F32, name="h%d" % (b % 4))
-            for t in range(4):
+            for t in (0, 1, 2, 3) if VECTOR_M[e] >= P else (2, 3, 0, 1):
                 nc.tensor.matmul_mx(
                     out=h_banks[b][:, t, :],
                     lhsT=waq[:, e, t * P : (t + 1) * P].bitcast(FP8X4),
@@ -166,12 +172,12 @@ def tile_moe_elr_silu_kernel(tc, x_words, x_scales, w_words, w_scales, wa, wb_wo
                 in_=hb[e][:, s0:s1, :].rearrange("p s t -> p (s t)"),
             )
 
-        def frozen(bank, f, b0, b, start):
-            words, scales = tokens_of(b)
+        def frozen(bank, f, b0, c0, c1, start):
+            words, scales = tokens_of(c0, c1)
             nc.tensor.matmul_mx(
-                out=bank[:, (b - b0) * P : (b - b0 + 1) * P],
-                lhsT=wt[:, b // 2, 2 * f * P : 2 * (f + 1) * P].bitcast(FP4X4),
-                lhsT_scale=wst[:, b // 2, f * P : (f + 1) * P],
+                out=bank[:, (c0 - b0) * P : (c1 - b0) * P],
+                lhsT=wt[:, c0 // 2, 2 * f * P : 2 * (f + 1) * P].bitcast(FP4X4),
+                lhsT_scale=wst[:, c0 // 2, f * P : (f + 1) * P],
                 rhs=words,
                 rhs_scale=scales,
                 start=start,
@@ -192,18 +198,18 @@ def tile_moe_elr_silu_kernel(tc, x_words, x_scales, w_words, w_scales, wa, wb_wo
 
         def upper_rows(name, b0, b1, engine_copy):
             bank = psum.tile([P, (b1 - b0) * P], F32, name=name)
-            for b in range(b0, b1):
-                frozen(bank, 0, b0, b, b == b0)
-            for e in range(b0 // 2, (b1 + 1) // 2):
-                c0, c1 = max(b0, 2 * e), min(b1, 2 * e + 2)
+            by_expert = [(max(b0, 2 * e), min(b1, 2 * e + 2)) for e in range(b0 // 2, (b1 + 1) // 2)]
+            for c0, c1 in by_expert:
+                frozen(bank, 0, b0, c0, c1, c0 == b0)
+            for c0, c1 in by_expert:
                 adapter(bank, 0, b0, c0, c1, False, c1 == b1)
             engine_copy(y[0][:, b0 * P : b1 * P], bank[:])
 
         def lower_rows(name, b0):
             bank = psum.tile([P, 4 * P], F32, name=name)
             adapter(bank, 1, b0, b0, b0 + 2, True, False)
-            for b in range(b0, b0 + 4):
-                frozen(bank, 1, b0, b, False)
+            frozen(bank, 1, b0, b0, b0 + 2, False)
+            frozen(bank, 1, b0, b0 + 2, b0 + 4, False)
             adapter(bank, 1, b0, b0 + 2, b0 + 4, False, True)
             nc.scalar.copy(y[1][:, b0 * P : (b0 + 4) * P], bank[:])
 
@@ -224,54 +230,51 @@ def tile_moe_elr_silu_kernel(tc, x_words, x_scales, w_words, w_scales, wa, wb_wo
         silu(7)
         quant_h(0, 2)
         quant_h(2, 4)
-        nc.vector.tensor_copy(gate_cols[:], turned_gate[:, 0:8])
+        nc.vector.tensor_copy(gate_cols[:], turned_gate[:, 0:2])
         quant_h(4, 6)
         quant_h(6, 7)
         quant_h(7, 8)
-        upper_rows("ya", 0, 4, nc.scalar.copy)
-        upper_rows("yb", 4, 7, nc.vector.tensor_copy)
-        upper_rows("yc", 7, 8, nc.scalar.copy)
+        upper_rows("ya", 0, 4, nc.vector.tensor_copy)
+        upper_rows("yb", 4, 7, nc.scalar.copy)
+        upper_rows("yc", 7, 8, nc.vector.tensor_copy)
         lower_rows("yd", 0)
         lower_rows("h0", 4)
 
-        def tokens(r, k0, k1):
-            return pos_t[r][:, k0 * P // 16 : k1 * P // 16]
+        gated = [[kept([P, T], F32, "gated%d%d" % (f, r)) for r in range(2)] for f in range(2)]
+        plain = kept([P, HALF], F32, "plain")
+        turned = kept([P, 4, P], F32, "turned")
+        res = [kept([P, T], F32, "res%d" % f) for f in range(2)]
 
-        def turn(picked, k0, k1, name):
-            turned = psum.tile([P, k1 - k0, P], F32, name=name)
-            for k in range(k0, k1):
-                nc.tensor.transpose(turned[:, k - k0, :], picked[:, k * P : (k + 1) * P], ident[:])
-            return turned
+        def picked(f, r, t0, t1):
+            return y[f][:].indirect(pos_t[r][:, t0 // 16 : t1 // 16])
 
-        def scale(r, turned, k0, k1):
-            for k in range(k0, k1):
-                nc.scalar.activation(scaled[r][:, k, :], turned[:, k - k0, :], COPY, scale=gate_cols[:, 4 * r + k : 4 * r + k + 1])
+        def fetch_gated(f, r, t0, t1):
+            nc.vector.tensor_tensor(gated[f][r][:, t0:t1], picked(f, r, t0, t1), gt[r][:, t0:t1], MULT)
 
-        def gated(f, r, k0, k1):
-            part = kept([P, (k1 - k0) * P], F32, "gated%d_%d_%d" % (r, f, k0))
-            nc.vector.tensor_tensor(part[:], y[f][:].indirect(tokens(r, k0, k1)), gt[:, r, k0 * P : k1 * P], MULT)
-            return part
+        gate_tail = psum.tile([P, HALF], F32, name="yd")
+        for k in range(2):
+            nc.tensor.transpose(gate_tail[:, k * P : (k + 1) * P], gate_cols[:, k : k + 1].to_broadcast([P, P]), ident[:])
+        nc.scalar.activation(plain[:], picked(1, 1, HALF, T), COPY)
 
-        picked = [kept([P, T], F32, "picked%d" % r) for r in range(2)]
-        scaled = [kept([P, 4, P], F32, "scaled%d" % r) for r in range(2)]
-        upper = kept([P, T], F32, "upper")
-        for r in range(2):
-            nc.vector.tensor_copy(picked[r][:], y[0][:].indirect(pos_t[r][:]))
-        for r, names in enumerate((("h2", "h3"), ("yc", "h1"))):
-            for b, name in enumerate(names):
-                scale(r, turn(picked[r], 2 * b, 2 * b + 2, name), 2 * b, 2 * b + 2)
-        back = [psum.tile([P, P], F32, name=name) for name in ("ya", "yb", "yd", "h0")]
-        for r in range(2):
-            for k in range(4):
-                nc.tensor.matmul(back[k][:], scaled[r][:, k, :], ident[:], start=r == 0, stop=r == 1, is_transpose=True)
-        for k in range(4):
-            nc.scalar.copy(upper[:, k * P : (k + 1) * P], back[k][:])
+        sums = [psum.tile([P, P], F32, name=name) for name in ("h1", "h2", "h3", "yc")]
+        for r, t0, t1 in ((0, 0, T), (1, 0, HALF), (1, HALF, T)):
+            fetch_gated(0, r, t0, t1)
+            for k in range(t0 // P, t1 // P):
+                nc.tensor.matmul(sums[k][:], gated[0][r][:, k * P : (k + 1) * P], ident[:], start=r == 0, stop=r == 1, is_transpose=True)
+        for b, name in enumerate(("ya", "yb")):
+            for k in range(2 * b, 2 * b + 2):
+                nc.scalar.copy(turned[:, k, :], sums[k][:])
+            back = psum.tile([P, HALF], F32, name=name)
+            for k in range(2):
+                nc.tensor.transpose(back[:, k * P : (k + 1) * P], turned[:, 2 * b + k, :], ident[:])
+            nc.scalar.copy(res[0][:, b * HALF : (b + 1) * HALF], back[:])
         for b in range(2):
-            nc.scalar.dma_start(out[0:P, 2 * b * P : 2 * (b + 1) * P], upper[:, 2 * b * P : 2 * (b + 1) * P])
+            nc.scalar.dma_start(out[0:P, b * HALF : (b + 1) * HALF], res[0][:, b * HALF : (b + 1) * HALF])
 
-        first = gated(1, 0, 0, 4)
-        second = [gated(1, 1, 2 * b, 2 * b + 2) for b in range(2)]
+        fetch_gated(1, 0, 0, T)
+        fetch_gated(1, 1, 0, HALF)
+        nc.vector.tensor_tensor(gated[1][1][:, HALF:T], plain[:], gate_tail[:], MULT)
         for b in range(2):
-            res = kept([P, 2 * P], F32, "res1_%d" % b)
-            nc.vector.tensor_tensor(res[:], first[:, 2 * b * P : 2 * (b + 1) * P], second[b][:], ADD)
-            nc.sync.dma_start(out[P : 2 * P, 2 * b * P : 2 * (b + 1) * P], res[:])
+            cols = slice(b * HALF, (b + 1) * HALF)
+            nc.vector.tensor_tensor(res[1][:, cols], gated[1][0][:, cols], gated[1][1][:, cols], ADD)
+            nc.sync.dma_start(out[P : 2 * P, cols], res[1][:, cols])

@@ -21,10 +21,9 @@ ADD = mybir.AluOpType.add
 
 P = 128
 S = E * C
-HALF = T // 2
 WINDOW = 704
 RAW = 16 * H
-VECTOR_M = (0, 104, 256, 188)
+VECTOR_M = (0, 104, 256, 196)
 GATHERS = ((0, 4), (4, 8))
 
 
@@ -55,14 +54,14 @@ def tile_moe_elr_silu_kernel(tc, x_words, x_scales, w_words, w_scales, wa, wb_wo
         wst = kept([P, E, N], U8, "wst")
         wbt = kept([P, E, N], I32, "wbt")
         wbst = kept([P, N], U8, "wbst")
-        gt = [kept([P, T], F32, "gt%d" % r) for r in range(2)]
+        gt = kept([P, 2, T], F32, "gt")
         hb = [placed([P, C, 4], BF16, "hb%d" % e, RAW if e == 0 else 4 * RAW) if e in (0, 2) else kept([P, C, 4], BF16, "hb%d" % e) for e in range(E)]
         hq = [placed([P, C], U32, "hq%d" % e, 3 * RAW + 8 * C + 4 * C * e) for e in range(2)] + [kept([P, C], U32, "hq%d" % e) for e in range(2, E)]
         hs = kept([P, S], U8, "hs")
         y = [kept([P, S], F32, "y%d" % f) for f in range(2)]
         ident = kept([P, P], F32, "ident")
         gate_rows = placed([P, P], F32, "gate_rows", 4 * RAW)
-        gate_cols = kept([P, 2], F32, "gate_cols")
+        gate_cols = kept([P, 8], F32, "gate_cols")
         zeros = kept([P, P], F32, "zeros")
 
         nc.gpsimd.memset(xs[:].bitcast(I32), 0)
@@ -89,7 +88,7 @@ def tile_moe_elr_silu_kernel(tc, x_words, x_scales, w_words, w_scales, wa, wb_wo
         load_x_scales(nc.sync, 3)
         for e in range(1, E):
             load_wa(e)
-        nc.sync.dma_start(gate_rows[0:2], gate[1, 0, HALF:T].rearrange("(k c) -> k c", c=P))
+        nc.sync.dma_start(gate_rows[0:8], gate[:, 0, :].rearrange("r (k c) -> r k c", c=P))
         for q in range(4):
             nc.sync.dma_start(
                 wst[32 * q : 32 * q + 4].bitcast(I32),
@@ -104,8 +103,7 @@ def tile_moe_elr_silu_kernel(tc, x_words, x_scales, w_words, w_scales, wa, wb_wo
             )
         nc.sync.dma_start(pos_t[0][:], pos1)
         nc.sync.dma_start(pos_t[1][:], pos2)
-        nc.sync.dma_start(gt[0][:], gate[0])
-        nc.sync.dma_start(gt[1][:], gate[1])
+        nc.sync.dma_start(gt[:], gate.rearrange("r p t -> p r t"))
 
         def gather(u):
             b0, b1 = GATHERS[u]
@@ -133,11 +131,11 @@ def tile_moe_elr_silu_kernel(tc, x_words, x_scales, w_words, w_scales, wa, wb_wo
             cast(nc.scalar.copy, e, 0, share, P)
 
         def quant_wa(e):
-            for t0 in (0, 2) if VECTOR_M[e] >= P else (2, 0):
+            for t0, t1 in ((0, 2), (2, 3), (3, 4)) if e == E - 1 else ((0, 2), (2, 4)) if VECTOR_M[e] >= P else ((2, 4), (0, 2)):
                 nc.vector.quantize_mx(
-                    out=waq[:, e, t0 * P : (t0 + 2) * P].bitcast(FP8X4),
-                    scales=was[:, e, t0 * P : (t0 + 2) * P],
-                    in_=wab[e][:, t0 : t0 + 2].rearrange("p t m j -> p (t m j)"),
+                    out=waq[:, e, t0 * P : t1 * P].bitcast(FP8X4),
+                    scales=was[:, e, t0 * P : t1 * P],
+                    in_=wab[e][:, t0:t1].rearrange("p t m j -> p (t m j)"),
                 )
 
         h_banks = {}
@@ -230,51 +228,54 @@ def tile_moe_elr_silu_kernel(tc, x_words, x_scales, w_words, w_scales, wa, wb_wo
         silu(7)
         quant_h(0, 2)
         quant_h(2, 4)
-        nc.vector.tensor_copy(gate_cols[:], turned_gate[:, 0:2])
+        nc.vector.tensor_copy(gate_cols[:], turned_gate[:, 0:8])
         quant_h(4, 6)
         quant_h(6, 7)
         quant_h(7, 8)
-        upper_rows("ya", 0, 4, nc.vector.tensor_copy)
-        upper_rows("yb", 4, 7, nc.scalar.copy)
-        upper_rows("yc", 7, 8, nc.vector.tensor_copy)
+        upper_rows("ya", 0, 4, nc.scalar.copy)
+        upper_rows("yb", 4, 7, nc.vector.tensor_copy)
+        upper_rows("yc", 7, 8, nc.scalar.copy)
         lower_rows("yd", 0)
         lower_rows("h0", 4)
 
-        gated = [[kept([P, T], F32, "gated%d%d" % (f, r)) for r in range(2)] for f in range(2)]
-        plain = kept([P, HALF], F32, "plain")
-        turned = kept([P, 4, P], F32, "turned")
-        res = [kept([P, T], F32, "res%d" % f) for f in range(2)]
+        def tokens(r, k0, k1):
+            return pos_t[r][:, k0 * P // 16 : k1 * P // 16]
 
-        def picked(f, r, t0, t1):
-            return y[f][:].indirect(pos_t[r][:, t0 // 16 : t1 // 16])
+        def turn(picked, k0, k1, name):
+            turned = psum.tile([P, k1 - k0, P], F32, name=name)
+            for k in range(k0, k1):
+                nc.tensor.transpose(turned[:, k - k0, :], picked[:, k * P : (k + 1) * P], ident[:])
+            return turned
 
-        def fetch_gated(f, r, t0, t1):
-            nc.vector.tensor_tensor(gated[f][r][:, t0:t1], picked(f, r, t0, t1), gt[r][:, t0:t1], MULT)
+        def scale(r, turned, k0, k1):
+            for k in range(k0, k1):
+                nc.scalar.activation(scaled[r][:, k, :], turned[:, k - k0, :], COPY, scale=gate_cols[:, 4 * r + k : 4 * r + k + 1])
 
-        gate_tail = psum.tile([P, HALF], F32, name="yd")
-        for k in range(2):
-            nc.tensor.transpose(gate_tail[:, k * P : (k + 1) * P], gate_cols[:, k : k + 1].to_broadcast([P, P]), ident[:])
-        nc.scalar.activation(plain[:], picked(1, 1, HALF, T), COPY)
+        def gated(f, r, k0, k1):
+            part = kept([P, (k1 - k0) * P], F32, "gated%d_%d_%d" % (r, f, k0))
+            nc.vector.tensor_tensor(part[:], y[f][:].indirect(tokens(r, k0, k1)), gt[:, r, k0 * P : k1 * P], MULT)
+            return part
 
-        sums = [psum.tile([P, P], F32, name=name) for name in ("h1", "h2", "h3", "yc")]
-        for r, t0, t1 in ((0, 0, T), (1, 0, HALF), (1, HALF, T)):
-            fetch_gated(0, r, t0, t1)
-            for k in range(t0 // P, t1 // P):
-                nc.tensor.matmul(sums[k][:], gated[0][r][:, k * P : (k + 1) * P], ident[:], start=r == 0, stop=r == 1, is_transpose=True)
-        for b, name in enumerate(("ya", "yb")):
-            for k in range(2 * b, 2 * b + 2):
-                nc.scalar.copy(turned[:, k, :], sums[k][:])
-            back = psum.tile([P, HALF], F32, name=name)
-            for k in range(2):
-                nc.tensor.transpose(back[:, k * P : (k + 1) * P], turned[:, 2 * b + k, :], ident[:])
-            nc.scalar.copy(res[0][:, b * HALF : (b + 1) * HALF], back[:])
+        picked = [kept([P, T], F32, "picked%d" % r) for r in range(2)]
+        scaled = [kept([P, 4, P], F32, "scaled%d" % r) for r in range(2)]
+        upper = kept([P, T], F32, "upper")
+        for r in range(2):
+            nc.vector.tensor_copy(picked[r][:], y[0][:].indirect(pos_t[r][:]))
+        for r, names in enumerate((("h2", "h3"), ("yc", "h1"))):
+            for b, name in enumerate(names):
+                scale(r, turn(picked[r], 2 * b, 2 * b + 2, name), 2 * b, 2 * b + 2)
+        back = [psum.tile([P, P], F32, name=name) for name in ("ya", "yb", "yd", "h0")]
+        for r in range(2):
+            for k in range(4):
+                nc.tensor.matmul(back[k][:], scaled[r][:, k, :], ident[:], start=r == 0, stop=r == 1, is_transpose=True)
+        for k in range(4):
+            nc.scalar.copy(upper[:, k * P : (k + 1) * P], back[k][:])
         for b in range(2):
-            nc.scalar.dma_start(out[0:P, b * HALF : (b + 1) * HALF], res[0][:, b * HALF : (b + 1) * HALF])
+            nc.scalar.dma_start(out[0:P, 2 * b * P : 2 * (b + 1) * P], upper[:, 2 * b * P : 2 * (b + 1) * P])
 
-        fetch_gated(1, 0, 0, T)
-        fetch_gated(1, 1, 0, HALF)
-        nc.vector.tensor_tensor(gated[1][1][:, HALF:T], plain[:], gate_tail[:], MULT)
+        first = gated(1, 0, 0, 4)
+        second = [gated(1, 1, 2 * b, 2 * b + 2) for b in range(2)]
         for b in range(2):
-            cols = slice(b * HALF, (b + 1) * HALF)
-            nc.vector.tensor_tensor(res[1][:, cols], gated[1][0][:, cols], gated[1][1][:, cols], ADD)
-            nc.sync.dma_start(out[P : 2 * P, cols], res[1][:, cols])
+            res = kept([P, 2 * P], F32, "res1_%d" % b)
+            nc.vector.tensor_tensor(res[:], first[:, 2 * b * P : 2 * (b + 1) * P], second[b][:], ADD)
+            nc.sync.dma_start(out[P : 2 * P, 2 * b * P : 2 * (b + 1) * P], res[:])

from contextlib import ExitStack

import concourse.mybir as mybir
from concourse.masks import make_identity

K, T, E, C, H, N = 512, 512, 4, 256, 512, 256
FLOPS = 2 * E * C * (K * H + K * N + H * N)

F32 = mybir.dt.float32
BF16 = mybir.dt.bfloat16
I32 = mybir.dt.int32
U32 = mybir.dt.uint32
U16 = mybir.dt.uint16
U8 = mybir.dt.uint8
FP8X4 = mybir.dt.float8_e4m3fn_x4
FP4X4 = mybir.dt.float4_e2m1fn_x4
COPY = mybir.ActivationFunctionType.Copy
SILU = mybir.ActivationFunctionType.Silu
MULT = mybir.AluOpType.mult
ADD = mybir.AluOpType.add

P = 128
S = E * C
WINDOW = 704
RAW = 16 * H
VECTOR_M = (0, 104, 256, 196)
GATHERS = ((0, 4), (4, 8))


def tile_moe_elr_silu_kernel(tc, x_words, x_scales, w_words, w_scales, wa, wb_words, wb_scales, gate, offs, pos1, pos2, out):
    nc = tc.nc
    with ExitStack() as ctx:
        keep = ctx.enter_context(tc.tile_pool(name="keep", bufs=1))
        shared = ctx.enter_context(tc.tile_pool(name="shared", bufs=1))
        psum = ctx.enter_context(tc.psum_pool(name="psum", bufs=1))

        def kept(shape, dtype, name):
            return keep.tile(shape, dtype, name=name, align_bytes=64)

        def placed(shape, dtype, name, offset):
            return shared.tile(shape, dtype, name=name, align_bytes=64, offset=offset)

        offs_t = keep.tile([P, S // 16], U16, name="offs_t")
        pos_t = [keep.tile([P, T // 16], U16, name="pos%d" % r) for r in range(2)]
        xw = kept([P, WINDOW], I32, "xw")
        xs = kept([P, WINDOW], U8, "xs")
        raw = [placed([P, 4, H], F32, "raw%d" % e, e * RAW) for e in range(E)]
        gw = [kept([P, (b1 - b0) * P], U32, "gw%d" % b0) for b0, b1 in GATHERS]
        gs = [kept([P, (b1 - b0) * P], U8, "gs%d" % b0) for b0, b1 in GATHERS]
        wab = [kept([P, 4, P, 4], BF16, "wab%d" % e) for e in range(E)]
        waq = kept([P, E, H], U32, "waq")
        was = kept([P, E, H], U8, "was")
        wt = kept([P, E, 2 * N], U8, "wt")
        wst = kept([P, E, N], U8, "wst")
        wbt = kept([P, E, N], I32, "wbt")
        wbst = kept([P, N], U8, "wbst")
        gt = kept([P, 2, T], F32, "gt")
        hb = [placed([P, C, 4], BF16, "hb%d" % e, RAW if e == 0 else 4 * RAW) if e in (0, 2) else kept([P, C, 4], BF16, "hb%d" % e) for e in range(E)]
        hq = [placed([P, C], U32, "hq%d" % e, 3 * RAW + 8 * C + 4 * C * e) for e in range(2)] + [kept([P, C], U32, "hq%d" % e) for e in range(2, E)]
        hs = kept([P, S], U8, "hs")
        y = [kept([P, S], F32, "y%d" % f) for f in range(2)]
        ident = kept([P, P], F32, "ident")
        gate_rows = placed([P, P], F32, "gate_rows", 4 * RAW)
        gate_cols = kept([P, 8], F32, "gate_cols")
        zeros = kept([P, P], F32, "zeros")

        nc.gpsimd.memset(xs[:].bitcast(I32), 0)
        nc.gpsimd.memset(wst[:].bitcast(I32), 0)
        nc.gpsimd.memset(wbst[:].bitcast(I32), 0)
        nc.vector.memset(xw[:, T:WINDOW], 0)
        nc.vector.memset(zeros[:], 0.0)

        def load_x_scales(queue, q):
            queue.dma_start(xs[32 * q : 32 * q + 4, 0:T].bitcast(I32), x_scales[0, 4 * q : 4 * q + 4, :].bitcast(I32))

        load_x_scales(nc.scalar, 0)
        load_x_scales(nc.scalar, 1)
        nc.scalar.activation(gate_rows[:], zeros[:], SILU)
        make_identity(nc, ident[:])

        def load_wa(e):
            nc.sync.dma_start(raw[e][:], wa[e].rearrange("(p j) i -> p j i", j=4))

        nc.sync.dma_start(xw[:, 0:T], x_words[0].rearrange("p t d -> p (t d)").bitcast(I32))
        nc.sync.dma_start(offs_t[:], offs)
        load_wa(0)
        load_x_scales(nc.sync, 2)
        load_x_scales(nc.sync, 3)
        for e in range(1, E):
            load_wa(e)
        nc.sync.dma_start(gate_rows[0:8], gate[:, 0, :].rearrange("r (k c) -> r k c", c=P))
        for q in range(4):
            nc.sync.dma_start(
                wst[32 * q : 32 * q + 4].bitcast(I32),
                w_scales[:, 0, 4 * q : 4 * q + 4, :].bitcast(I32).rearrange("e r n -> r e n"),
            )
        nc.sync.dma_start(wt[:].bitcast(I32), w_words[:, 0].bitcast(I32).rearrange("e p b -> p e b"))
        nc.sync.dma_start(wbt[:], wb_words[:, 0].rearrange("e p n d -> p e (n d)").bitcast(I32))
        for q in range(4):
            nc.sync.dma_start(
                wbst[32 * q : 32 * q + 16].bitcast(I32),
                wb_scales[:, 0, 4 * q : 4 * q + 4, :].bitcast(I32),
            )
        nc.sync.dma_start(pos_t[0][:], pos1)
        nc.sync.dma_start(pos_t[1][:], pos2)
        nc.sync.dma_start(gt[:], gate.rearrange("r p t -> p r t"))

        def gather(u):
            b0, b1 = GATHERS[u]
            lst = offs_t[:, b0 * P // 16 : b1 * P // 16]
            nc.vector.tensor_copy(gw[u][:], xw[:].bitcast(U32).indirect(lst))
            nc.vector.tensor_copy(gs[u][:], xs[:].indirect(lst))

        def tokens_of(c0, c1):
            u = [b0 <= c0 < b1 for b0, b1 in GATHERS].index(True)
            cols = slice((c0 - GATHERS[u][0]) * P, (c1 - GATHERS[u][0]) * P)
            return gw[u][:, cols].bitcast(FP8X4), gs[u][:, cols]

        def cast(engine_copy, e, t0, m0, m1):
            if m1 > m0:
                engine_copy(
                    wab[e][:, t0 : t0 + 2, m0:m1, :].rearrange("p t m j -> p m j t"),
                    raw[e][:, :, 4 * m0 : 4 * m1].rearrange("p j (m t) -> p m j t", t=4)[:, :, :, t0 : t0 + 2],
                )

        def cast_wa(e):
            share = VECTOR_M[e]
            cast(nc.vector.tensor_copy, e, 0, 0, min(share, P))
            cast(nc.vector.tensor_copy, e, 2, 0, share - P)
            cast(nc.scalar.copy, e, 2, max(share - P, 0), P)
            cast(nc.scalar.copy, e, 0, share, P)

        def quant_wa(e):
            for t0, t1 in ((0, 2), (2, 3), (3, 4)) if e == E - 1 else ((0, 2), (2, 4)) if VECTOR_M[e] >= P else ((2, 4), (0, 2)):
                nc.vector.quantize_mx(
                    out=waq[:, e, t0 * P : t1 * P].bitcast(FP8X4),
                    scales=was[:, e, t0 * P : t1 * P],
                    in_=wab[e][:, t0:t1].rearrange("p t m j -> p (t m j)"),
                )

        h_banks = {}

        def first_layer(b):
            e = b // 2
            words, scales = tokens_of(b, b + 1)
            h_banks[b] = psum.tile([P, 4, P], F32, name="h%d" % (b % 4))
            for t in (0, 1, 2, 3) if VECTOR_M[e] >= P else (2, 3, 0, 1):
                nc.tensor.matmul_mx(
                    out=h_banks[b][:, t, :],
                    lhsT=waq[:, e, t * P : (t + 1) * P].bitcast(FP8X4),
                    lhsT_scale=was[:, e, t * P : (t + 1) * P],
                    rhs=words,
                    rhs_scale=scales,
                    start=True,
                    stop=True,
                )

        def silu(b):
            nc.scalar.activation(
                hb[b // 2][:, b % 2 * P : (b % 2 + 1) * P, :].rearrange("p (s v) t -> p s t v", v=2),
                h_banks[b][:].rearrange("p t (s v) -> p s t v", v=2),
                SILU,
            )

        def quant_h(b0, b1):
            e, s0, s1 = b0 // 2, b0 % 2 * P, (b1 - b0 + b0 % 2) * P
            nc.vector.quantize_mx(
                out=hq[e][:, s0:s1].bitcast(FP8X4),
                scales=hs[:, b0 * P : b1 * P],
                in_=hb[e][:, s0:s1, :].rearrange("p s t -> p (s t)"),
            )

        def frozen(bank, f, b0, c0, c1, start):
            words, scales = tokens_of(c0, c1)
            nc.tensor.matmul_mx(
                out=bank[:, (c0 - b0) * P : (c1 - b0) * P],
                lhsT=wt[:, c0 // 2, 2 * f * P : 2 * (f + 1) * P].bitcast(FP4X4),
                lhsT_scale=wst[:, c0 // 2, f * P : (f + 1) * P],
                rhs=words,
                rhs_scale=scales,
                start=start,
                stop=False,
            )

        def adapter(bank, f, b0, c0, c1, start, stop):
            e = c0 // 2
            nc.tensor.matmul_mx(
                out=bank[:, (c0 - b0) * P : (c1 - b0) * P],
                lhsT=wbt[:, e, f * P : (f + 1) * P].bitcast(FP8X4),
                lhsT_scale=wbst[4 * e :, f * P : (f + 1) * P],
                rhs=hq[e][:, (c0 - 2 * e) * P : (c1 - 2 * e) * P].bitcast(FP8X4),
                rhs_scale=hs[:, c0 * P : c1 * P],
                start=start,
                stop=stop,
            )

        def upper_rows(name, b0, b1, engine_copy):
            bank = psum.tile([P, (b1 - b0) * P], F32, name=name)
            by_expert = [(max(b0, 2 * e), min(b1, 2 * e + 2)) for e in range(b0 // 2, (b1 + 1) // 2)]
            for c0, c1 in by_expert:
                frozen(bank, 0, b0, c0, c1, c0 == b0)
            for c0, c1 in by_expert:
                adapter(bank, 0, b0, c0, c1, False, c1 == b1)
            engine_copy(y[0][:, b0 * P : b1 * P], bank[:])

        def lower_rows(name, b0):
            bank = psum.tile([P, 4 * P], F32, name=name)
            adapter(bank, 1, b0, b0, b0 + 2, True, False)
            frozen(bank, 1, b0, b0, b0 + 2, False)
            frozen(bank, 1, b0, b0 + 2, b0 + 4, False)
            adapter(bank, 1, b0, b0 + 2, b0 + 4, False, True)
            nc.scalar.copy(y[1][:, b0 * P : (b0 + 4) * P], bank[:])

        gather(0)
        gather(1)
        for e in range(E):
            cast_wa(e)
            if e == E - 1:
                turned_gate = psum.tile([P, P], F32, name="yd")
                nc.tensor.transpose(turned_gate[:], gate_rows[:], ident[:])
            if e > 0:
                silu(2 * e - 2)
                silu(2 * e - 1)
            quant_wa(e)
            first_layer(2 * e)
            first_layer(2 * e + 1)
        silu(6)
        silu(7)
        quant_h(0, 2)
        quant_h(2, 4)
        nc.vector.tensor_copy(gate_cols[:], turned_gate[:, 0:8])
        quant_h(4, 6)
        quant_h(6, 7)
        quant_h(7, 8)
        upper_rows("ya", 0, 4, nc.scalar.copy)
        upper_rows("yb", 4, 7, nc.vector.tensor_copy)
        upper_rows("yc", 7, 8, nc.scalar.copy)
        lower_rows("yd", 0)
        lower_rows("h0", 4)

        def tokens(r, k0, k1):
            return pos_t[r][:, k0 * P // 16 : k1 * P // 16]

        def turn(picked, k0, k1, name):
            turned = psum.tile([P, k1 - k0, P], F32, name=name)
            for k in range(k0, k1):
                nc.tensor.transpose(turned[:, k - k0, :], picked[:, k * P : (k + 1) * P], ident[:])
            return turned

        def scale(r, turned, k0, k1):
            for k in range(k0, k1):
                nc.scalar.activation(scaled[r][:, k, :], turned[:, k - k0, :], COPY, scale=gate_cols[:, 4 * r + k : 4 * r + k + 1])

        def gated(f, r, k0, k1):
            part = kept([P, (k1 - k0) * P], F32, "gated%d_%d_%d" % (r, f, k0))
            nc.vector.tensor_tensor(part[:], y[f][:].indirect(tokens(r, k0, k1)), gt[:, r, k0 * P : k1 * P], MULT)
            return part

        picked = [kept([P, T], F32, "picked%d" % r) for r in range(2)]
        scaled = [kept([P, 4, P], F32, "scaled%d" % r) for r in range(2)]
        upper = kept([P, T], F32, "upper")
        for r in range(2):
            nc.vector.tensor_copy(picked[r][:], y[0][:].indirect(pos_t[r][:]))
        for r, names in enumerate((("h2", "h3"), ("yc", "h1"))):
            for b, name in enumerate(names):
                scale(r, turn(picked[r], 2 * b, 2 * b + 2, name), 2 * b, 2 * b + 2)
        back = [psum.tile([P, P], F32, name=name) for name in ("ya", "yb", "yd", "h0")]
        for r in range(2):
            for k in range(4):
                nc.tensor.matmul(back[k][:], scaled[r][:, k, :], ident[:], start=r == 0, stop=r == 1, is_transpose=True)
        for k in range(4):
            nc.scalar.copy(upper[:, k * P : (k + 1) * P], back[k][:])
        for b in range(2):
            nc.scalar.dma_start(out[0:P, 2 * b * P : 2 * (b + 1) * P], upper[:, 2 * b * P : 2 * (b + 1) * P])

        first = gated(1, 0, 0, 4)
        second = [gated(1, 1, 2 * b, 2 * b + 2) for b in range(2)]
        for b in range(2):
            res = kept([P, 2 * P], F32, "res1_%d" % b)
            nc.vector.tensor_tensor(res[:], first[:, 2 * b * P : 2 * (b + 1) * P], second[b][:], ADD)
            nc.sync.dma_start(out[P : 2 * P, 2 * b * P : 2 * (b + 1) * P], res[:])
